import numpy as np
import ml_dtypes


def mxq(x, axis, fmt="e4m3"):
    dtype, down = {"e4m3": (ml_dtypes.float8_e4m3fn, 7), "e5m2": (ml_dtypes.float8_e5m2, 14)}[fmt]
    v = np.moveaxis(np.asarray(x, np.float32).astype(ml_dtypes.bfloat16).astype(np.float64), axis, -1)
    blocks = v.reshape(v.shape[:-1] + (-1, 32))
    amax = np.abs(blocks).max(-1, keepdims=True)
    byte = np.maximum(np.where(amax > 0, np.frexp(amax)[1] - 1 + 127, 0) - down, 1)
    scale = np.exp2(byte - 127.0)
    codes = (blocks / scale).astype(np.float32).astype(dtype).astype(np.float64)
    return np.moveaxis((codes * scale).reshape(v.shape), -1, axis)


WIDE = False


def mx_kscale(k):
    if not WIDE:
        return np.ones(k)
    levels = np.array([10, -10, 5, -5, 0])
    if k % 512:
        return np.exp2(np.random.permutation(np.resize(levels, k // 32))).repeat(32)
    a = np.empty((k // 512, 16))
    for p in range(k // 512):
        a[p, :8] = np.random.permutation(np.resize(levels, 8))
        for g in range(8):
            far = levels[np.abs(levels - a[p, g]) >= 10]
            a[p, g + 8] = far[np.random.randint(len(far))]
    return np.exp2(a.ravel()).repeat(32)


def f64(x):
    return np.asarray(x).astype(np.float64)


def striped(idx):
    return np.tile(idx.reshape(-1, 16).T, (8, 1)).astype(np.uint16)


def unstriped(offs):
    return offs[:16].T.reshape(-1).astype(np.int64)


def striped8(idx):
    return np.concatenate([x.reshape(-1, 16).T for x in idx]).astype(np.uint16)


def runs(offs, k):
    lists = np.stack([offs[16 * r : 16 * r + 16].T.reshape(-1) for r in range(8)]).astype(np.int64)
    return lists[np.arange(k) % 512 // 64]


def pack_weight(w):
    k, n = w.shape
    w = f64(np.asarray(w, np.float32).astype(ml_dtypes.bfloat16)).reshape(k // 32, 32, n)
    amax = np.abs(w).max(1)
    byte = np.clip(np.where(amax > 0, np.frexp(amax)[1] - 1 + 127 - 7, 1), 1, 254)
    scaled = (w * np.exp2(127.0 - byte)[:, None, :]).reshape(k, n).astype(np.float32)
    words = np.ascontiguousarray(scaled.reshape(k // 512, 128, 4, n).transpose(0, 1, 3, 2)).astype(ml_dtypes.float8_e4m3fn).view(np.uint8)
    return words, np.ascontiguousarray(byte.astype(np.uint8).reshape(k // 512, 16, n))


def unpack_weight(words, scales):
    g, p, n, _ = words.shape
    vals = np.ascontiguousarray(words).view(ml_dtypes.float8_e4m3fn).astype(np.float64) * np.repeat(np.exp2(scales.astype(np.float64) - 127.0), 8, axis=1)[..., None]
    return vals.transpose(0, 1, 3, 2).reshape(g * 512, n)


def sigmoid(v):
    return 1.0 / (1.0 + np.exp(-np.maximum(v, -700.0)))

def planes(y):
    n, m = y.shape
    v = y.astype(np.float32).astype(ml_dtypes.bfloat16).astype(np.float64).reshape(n // 32, 32, m)
    top = np.abs(v).max(1)
    byte = np.clip(np.where(top > 0, np.frexp(top)[1] - 1 + 127 - 7, 1), 1, 254)
    codes = (v * np.exp2(127.0 - byte)[:, None, :]).reshape(n, m).astype(np.float32).astype(ml_dtypes.float8_e4m3fn).view(np.uint8)
    words = codes.reshape(n // 512, 128, 4, m).transpose(0, 1, 3, 2)
    return np.ascontiguousarray(words), np.ascontiguousarray(byte.astype(np.uint8).reshape(n // 512, 16, m))


K, T, S, N, H = 512, 2048, 512, 512, 512


def setup_inputs():
    n = np.random.standard_normal
    s = mx_kscale(K)[:, None]
    u = mx_kscale(H)
    packed_xT = pack_weight(n((K, T)) * s)
    packed_w1 = pack_weight(n((K, H)) / np.sqrt(K) / s)
    packed_w3 = pack_weight(n((H, N)) / np.sqrt(H) / u[:, None])
    return {
        "x_words": packed_xT[0],
        "x_scales": packed_xT[1],
        "w1_words": packed_w1[0],
        "w1_scales": packed_w1[1],
        "w2": (n((K, H)) / np.sqrt(K) / s * u).astype(np.float32),
        "w3_words": packed_w3[0],
        "w3_scales": packed_w3[1],
        "offs": striped(np.random.permutation(T)[:S]),
        "tap": striped8(np.stack([np.random.permutation(S) for _ in range(8)])),
    }


def reference(x_words, x_scales, w1_words, w1_scales, w2, w3_words, w3_scales, offs, tap):
    xq = unpack_weight(x_words, x_scales)[:, unstriped(offs)]
    e = mxq(f64(w2), 0, "e4m3").T @ xq
    y = unpack_weight(w1_words, w1_scales).T @ xq
    z = (e + e[np.arange(H)[:, None], runs(tap, H)]) * (sigmoid(y + y[np.arange(H)[:, None], runs(tap, H)]))
    out_0 = unpack_weight(w3_words, w3_scales).T @ mxq(z, 0, "e4m3")
    return (out_0,) + planes(out_0)

@@ -1,0 +1,243 @@
+from contextlib import ExitStack
+
+import concourse.mybir as mybir
+
+F32 = mybir.dt.float32
+BF16 = mybir.dt.bfloat16
+I32 = mybir.dt.int32
+U32 = mybir.dt.uint32
+U16 = mybir.dt.uint16
+U8 = mybir.dt.uint8
+FP8X4 = mybir.dt.float8_e4m3fn_x4
+ADD = mybir.AluOpType.add
+MULT = mybir.AluOpType.mult
+SIGMOID = mybir.ActivationFunctionType.Sigmoid
+
+P = 128
+PACK = 4
+T, S, H = 2048, 512, 512
+HALF = S // 2
+UNIT = 128
+FLOPS = 3 * 2 * 512 * 512 * 512
+CHUNKS = ((0, 256), (256, 384), (384, 512))
+
+
+def tile_picked_glutap_none_po_kernel(
+    tc, x_words, x_scales, w1_words, w1_scales, w2, w3_words, w3_scales, offs, tap, out_0, out_1, out_2
+):
+    nc = tc.nc
+    with ExitStack() as ctx:
+        keep = ctx.enter_context(tc.tile_pool(name="keep", bufs=1))
+        psum = ctx.enter_context(tc.psum_pool(name="psum", bufs=1))
+
+        def sb(name, shape, dtype):
+            return keep.tile(shape, dtype, name=name, align_bytes=64)
+
+        def words_view(dram):
+            return dram[0].rearrange("p n t -> p (n t)").bitcast(I32)
+
+        def load_scale_rows(queue, plane, dram):
+            for q in range(4):
+                queue.dma_start(plane[32 * q : 32 * q + 4, :].bitcast(I32), dram[0, 4 * q : 4 * q + 4, :].bitcast(I32))
+
+        def entries(lists, a, b):
+            return lists[:, a // 16 : b // 16]
+
+        offs_sb = keep.tile([P, S // 16], U16, name="offs_sb")
+        tap_sb = keep.tile([P, S // 16], U16, name="tap_sb")
+        x_tab = sb("x_tab", [P, T], U32)
+        xs_tab = sb("xs_tab", [P, T], U8)
+        w1_raw = sb("w1_raw", [P, H], U32)
+        w3_raw = sb("w3_raw", [P, H], U32)
+        w1s_raw = sb("w1s_raw", [P, H], U8)
+        w3s_raw = sb("w3s_raw", [P, H], U8)
+        w2_raw = [sb(f"w2_raw{h}", [P, PACK, HALF], F32) for h in range(2)]
+        warm = sb("warm", [P, 16], F32)
+        warm_out = sb("warm_out", [P, 16], F32)
+
+        nc.vector.memset(xs_tab[:].bitcast(I32), 0)
+        nc.vector.memset(warm[:], 0.0)
+        nc.vector.memset(w1s_raw[:].bitcast(I32), 0)
+        nc.vector.memset(w3s_raw[:].bitcast(I32), 0)
+
+        w2_rows = w2.rearrange("(p j) c -> p j c", j=PACK)
+        nc.sync.dma_start(offs_sb[:], offs)
+        nc.sync.dma_start(w2_raw[0][:], w2_rows[:, :, 0:HALF])
+        load_scale_rows(nc.sync, xs_tab, x_scales)
+        nc.sync.dma_start(w2_raw[1][:], w2_rows[:, :, HALF:H])
+        nc.sync.dma_start(x_tab[:].bitcast(I32), words_view(x_words))
+        nc.sync.dma_start(w1_raw[:].bitcast(I32), words_view(w1_words))
+        load_scale_rows(nc.sync, w1s_raw, w1_scales)
+        nc.sync.dma_start(w3_raw[:].bitcast(I32), words_view(w3_words))
+        nc.sync.dma_start(tap_sb[:], tap)
+        load_scale_rows(nc.sync, w3s_raw, w3_scales)
+        nc.scalar.activation(warm_out[:], warm[:], SIGMOID)
+
+        xs = sb("xs", [P, S], U8)
+        nc.vector.tensor_copy(xs[:], xs_tab[:].indirect(offs_sb[:]))
+
+        w2_bf = sb("w2_bf", [P, PACK, P, PACK], BF16)
+        for h in range(2):
+            dst = w2_bf[:, :, 64 * h : 64 * h + 64, :].rearrange("p t m j -> p m t j")
+            src = w2_raw[h][:].rearrange("p j (m t) -> p m t j", t=PACK)
+            if h == 0:
+                nc.scalar.copy(dst, src)
+            else:
+                nc.vector.tensor_copy(dst, src)
+
+        def deal(name, raw, dtype):
+            dealt = sb(name, [P, PACK, P], dtype)
+            nc.vector.tensor_copy(dealt[:].rearrange("p t m -> p m t"), raw[:].rearrange("p (m t) -> p m t", t=PACK))
+            return dealt
+
+        w2q = sb("w2q", [P, PACK, P], U32)
+        w2s = sb("w2s", [P, PACK, P], U8)
+        nc.vector.quantize_mx(
+            out=w2q[:].rearrange("p t m -> p (t m)").bitcast(FP8X4),
+            scales=w2s[:].rearrange("p t m -> p (t m)"),
+            in_=w2_bf[:].rearrange("p t m j -> p (t m j)"),
+        )
+
+        xq = sb("xq", [P, S], U32)
+        for h in range(2):
+            a, b = h * HALF, (h + 1) * HALF
+            nc.vector.tensor_copy(xq[:, a:b], x_tab[:].indirect(entries(offs_sb, a, b)))
+
+        def project(wq, ws, t, a, b, k):
+            bank = psum.tile([P, S], F32, name=f"bank{k}")
+            nc.tensor.matmul_mx(
+                bank[:, 0 : b - a],
+                lhsT=wq[:, t, :].bitcast(FP8X4),
+                lhsT_scale=ws[:, t, :],
+                rhs=xq[:, a:b].bitcast(FP8X4),
+                rhs_scale=xs[:, a:b],
+                start=True,
+                stop=True,
+            )
+            return bank
+
+        e_win = [sb(f"e_win{t}", [P, S], F32) for t in range(PACK)]
+        e_dup = [sb(f"e_dup{t}", [P, S], F32) for t in range(PACK)]
+        y_win = [sb(f"y_win{t}", [P, S], F32) for t in range(PACK)]
+        y_dup = [None] + [sb(f"y_dup{t}", [P, S], F32) for t in range(1, PACK)]
+        y_sum = sb("y_sum", [P, PACK, S], F32)
+        gate = sb("gate", [P, PACK, S], F32)
+        e_ring = sb("e_ring", [P, len(CHUNKS) - 1 + PACK, HALF], F32)
+        e_sum = []
+        for c, (a, b) in enumerate(CHUNKS):
+            first = len(CHUNKS) - 1 - c
+            e_sum.append(e_ring[:, first : first + PACK, 0 : b - a])
+
+        def tap_add(dst, win, dup, a, b):
+            nc.vector.tensor_tensor(dst, win[:].indirect(entries(tap_sb, a, b)), dup[:, a:b], ADD)
+
+        for h in range(2):
+            a, b = h * HALF, (h + 1) * HALF
+            bank = project(w2q, w2s, 0, a, b, h)
+            nc.scalar.copy(e_win[0][:, a:b], bank[:, 0:HALF])
+            nc.scalar.copy(e_dup[0][:, a:b], bank[:, 0:HALF])
+
+        w1q = deal("w1q", w1_raw, U32)
+        w1s = deal("w1s", w1s_raw, U8)
+        w3q = deal("w3q", w3_raw, U32)
+        w3s = deal("w3s", w3s_raw, U8)
+
+        for c, (a, b) in enumerate(CHUNKS):
+            tap_add(e_sum[c][:, 0, :], e_win[0], e_dup[0], a, b)
+
+        y_bank = {}
+        for k, t in enumerate((0, 2, 1, 3)):
+            y_bank[t] = project(w1q, w1s, t, 0, S, 2 + k)
+            nc.scalar.copy(y_win[t][:], y_bank[t][:])
+            if t == 0:
+                y_dup[0] = sb("e_dup0", [P, S], F32)
+                nc.vector.tensor_copy(y_dup[t][:], y_win[t][:])
+            elif t != 1:
+                nc.sync.dma_start(y_dup[t][:], y_win[t][:])
+        for h in range(2):
+            a, b = h * HALF, (h + 1) * HALF
+            nc.scalar.copy(y_dup[1][:, a:b], y_bank[1][:, a:b])
+        for t in range(1, PACK):
+            bank = project(w2q, w2s, t, 0, S, 1 + t)
+            nc.scalar.copy(e_win[t][:], bank[:])
+            nc.sync.dma_start(e_dup[t][:], e_win[t][:])
+
+        for t in range(PACK):
+            for h in range(2):
+                a, b = h * HALF, (h + 1) * HALF
+                tap_add(y_sum[:, t, a:b], y_win[t], y_dup[t], a, b)
+            nc.scalar.activation(gate[:, t, :], y_sum[:, t, :], SIGMOID)
+
+        oq = sb("oq", [P, S], U32)
+        osc = sb("osc", [P, S], U8)
+        out_rows = out_0.rearrange("(p t) n -> p t n", t=PACK)
+        out_words = words_view(out_1)
+        z_bf = [sb(f"z_bf{c}", [P, b - a, PACK], BF16) for c, (a, b) in enumerate(CHUNKS)]
+        zq = [sb(f"zq{c}", [P, b - a], U32) for c, (a, b) in enumerate(CHUNKS)]
+        zs = [sb(f"zs{c}", [P, b - a], U8) for c, (a, b) in enumerate(CHUNKS)]
+        o_bf = [sb(f"o_bf{u}", [P, UNIT, PACK], BF16) for u in range(S // UNIT)]
+
+        def gather_e(c, t):
+            a, b = CHUNKS[c]
+            tap_add(e_sum[c][:, t, :], e_win[t], e_dup[t], a, b)
+
+        def gated(c):
+            a, b = CHUNKS[c]
+            nc.vector.tensor_tensor(
+                z_bf[c][:].rearrange("p (c i) t -> p c t i", i=4),
+                e_sum[c].rearrange("p t (c i) -> p c t i", i=4),
+                gate[:, :, a:b].rearrange("p t (c i) -> p c t i", i=4),
+                MULT,
+            )
+
+        def last_layer(c):
+            a, b = CHUNKS[c]
+            nc.vector.quantize_mx(
+                out=zq[c][:].bitcast(FP8X4), scales=zs[c][:], in_=z_bf[c][:].rearrange("p n t -> p (n t)")
+            )
+            for n0 in range(a, b, UNIT):
+                u = n0 // UNIT
+                bank = psum.tile([P, PACK, UNIT], F32, name=f"bank{(6 + u) % 8}")
+                for t in range(PACK):
+                    nc.tensor.matmul_mx(
+                        bank[:, t, :],
+                        lhsT=w3q[:, t, :].bitcast(FP8X4),
+                        lhsT_scale=w3s[:, t, :],
+                        rhs=zq[c][:, n0 - a : n0 - a + UNIT].bitcast(FP8X4),
+                        rhs_scale=zs[c][:, n0 - a : n0 - a + UNIT],
+                        start=True,
+                        stop=True,
+                    )
+                nc.scalar.copy(o_bf[u][:], bank[:].rearrange("p t n -> p n t"))
+                o_f32 = sb(f"o_f32{u}", [P, PACK, UNIT], F32)
+                nc.scalar.copy(o_f32[:], bank[:])
+                nc.sync.dma_start(out_rows[:, :, n0 : n0 + UNIT], o_f32[:])
+
+        def hand_on(u):
+            a, b = u * UNIT, (u + 1) * UNIT
+            nc.vector.quantize_mx(
+                out=oq[:, a:b].bitcast(FP8X4), scales=osc[:, a:b], in_=o_bf[u][:].rearrange("p n t -> p (n t)")
+            )
+            nc.sync.dma_start(out_words[:, a:b], oq[:, a:b].bitcast(I32))
+
+        for t in range(1, PACK):
+            gather_e(0, t)
+        gated(0)
+        gather_e(1, 1)
+        last_layer(0)
+        gather_e(1, 2)
+        gather_e(1, 3)
+        gated(1)
+        gather_e(2, 1)
+        last_layer(1)
+        gather_e(2, 2)
+        hand_on(0)
+        gather_e(2, 3)
+        gated(2)
+        hand_on(1)
+        last_layer(2)
+        hand_on(2)
+        hand_on(3)
+        for q in range(4):
+            queue = nc.scalar if q % 2 else nc.sync
+            queue.dma_start(out_2[0, 4 * q : 4 * q + 4, :].bitcast(I32), osc[32 * q : 32 * q + 4, :].bitcast(I32))

@@ -61,8 +61,8 @@ def tile_picked_glutap_none_po_kernel(
         nc.vector.memset(w3s_raw[:].bitcast(I32), 0)
 
         w2_rows = w2.rearrange("(p j) c -> p j c", j=PACK)
-        nc.sync.dma_start(offs_sb[:], offs)
         nc.sync.dma_start(w2_raw[0][:], w2_rows[:, :, 0:HALF])
+        nc.sync.dma_start(offs_sb[:], offs)
         load_scale_rows(nc.sync, xs_tab, x_scales)
         nc.sync.dma_start(w2_raw[1][:], w2_rows[:, :, HALF:H])
         nc.sync.dma_start(x_tab[:].bitcast(I32), words_view(x_words))
@@ -87,7 +87,12 @@ def tile_picked_glutap_none_po_kernel(
 
         def deal(name, raw, dtype):
             dealt = sb(name, [P, PACK, P], dtype)
-            nc.vector.tensor_copy(dealt[:].rearrange("p t m -> p m t"), raw[:].rearrange("p (m t) -> p m t", t=PACK))
+            if dtype == U8:
+                nc.vector.tensor_copy(dealt[:], raw[:].rearrange("p (m t) -> p t m", t=PACK))
+            else:
+                nc.vector.tensor_copy(
+                    dealt[:].rearrange("p t m -> p m t"), raw[:].rearrange("p (m t) -> p m t", t=PACK)
+                )
             return dealt
 
         w2q = sb("w2q", [P, PACK, P], U32)
@@ -117,55 +122,54 @@ def tile_picked_glutap_none_po_kernel(
             return bank
 
         e_win = [sb(f"e_win{t}", [P, S], F32) for t in range(PACK)]
-        e_dup = [sb(f"e_dup{t}", [P, S], F32) for t in range(PACK)]
-        y_win = [sb(f"y_win{t}", [P, S], F32) for t in range(PACK)]
-        y_dup = [None] + [sb(f"y_dup{t}", [P, S], F32) for t in range(1, PACK)]
         y_sum = sb("y_sum", [P, PACK, S], F32)
         gate = sb("gate", [P, PACK, S], F32)
-        e_ring = sb("e_ring", [P, len(CHUNKS) - 1 + PACK, HALF], F32)
-        e_sum = []
-        for c, (a, b) in enumerate(CHUNKS):
-            first = len(CHUNKS) - 1 - c
-            e_sum.append(e_ring[:, first : first + PACK, 0 : b - a])
+        e_ring = sb("e_ring", [P, 1 + PACK, HALF], F32)
+        e_sum = [e_ring[:, 1 : 1 + PACK, :], e_ring[:, 0:PACK, 0:UNIT], e_ring[:, 0:PACK, UNIT:HALF]]
 
-        def tap_add(dst, win, dup, a, b):
-            nc.vector.tensor_tensor(dst, win[:].indirect(entries(tap_sb, a, b)), dup[:, a:b], ADD)
+        def tap_add(dst, win, plain, a, b):
+            nc.vector.tensor_tensor(dst, win[:].indirect(entries(tap_sb, a, b)), plain, ADD)
 
+        y_win = {t: sb(f"y_win{t}", [P, 2 * S], F32) for t in (0, 2, 3)}
+        e0_dup = y_win[0][:, S : 2 * S]
         for h in range(2):
             a, b = h * HALF, (h + 1) * HALF
             bank = project(w2q, w2s, 0, a, b, h)
             nc.scalar.copy(e_win[0][:, a:b], bank[:, 0:HALF])
-            nc.scalar.copy(e_dup[0][:, a:b], bank[:, 0:HALF])
+            nc.scalar.copy(e0_dup[:, a:b], bank[:, 0:HALF])
 
         w1q = deal("w1q", w1_raw, U32)
         w1s = deal("w1s", w1s_raw, U8)
-        w3q = deal("w3q", w3_raw, U32)
-        w3s = deal("w3s", w3s_raw, U8)
 
-        for c, (a, b) in enumerate(CHUNKS):
-            tap_add(e_sum[c][:, 0, :], e_win[0], e_dup[0], a, b)
+        for h in range(2):
+            a, b = h * HALF, (h + 1) * HALF
+            tap_add(e_ring[:, 1 - h, :], e_win[0], e0_dup[:, a:b], a, b)
 
+        y_win[1] = sb("e_win0", [P, 2 * S], F32)
+        y3_dup = sb("y3_dup", [P, S], F32)
+        y_dup = [y_win[t + 1][:, S : 2 * S] for t in range(PACK - 1)] + [y3_dup[:]]
         y_bank = {}
         for k, t in enumerate((0, 2, 1, 3)):
             y_bank[t] = project(w1q, w1s, t, 0, S, 2 + k)
-            nc.scalar.copy(y_win[t][:], y_bank[t][:])
+            nc.scalar.copy(y_win[t][:, 0:S], y_bank[t][:])
             if t == 0:
-                y_dup[0] = sb("e_dup0", [P, S], F32)
-                nc.vector.tensor_copy(y_dup[t][:], y_win[t][:])
+                nc.vector.tensor_copy(y_dup[t], y_win[t][:, 0:S])
             elif t != 1:
-                nc.sync.dma_start(y_dup[t][:], y_win[t][:])
+                nc.sync.dma_start(y_dup[t], y_win[t][:, 0:S])
         for h in range(2):
             a, b = h * HALF, (h + 1) * HALF
             nc.scalar.copy(y_dup[1][:, a:b], y_bank[1][:, a:b])
+        e_dup = {}
         for t in range(1, PACK):
             bank = project(w2q, w2s, t, 0, S, 1 + t)
             nc.scalar.copy(e_win[t][:], bank[:])
-            nc.sync.dma_start(e_dup[t][:], e_win[t][:])
+            for h in range(2):
+                e_dup[t, h] = sb(f"e_dup{t}_{h}", [P, HALF], F32)
+                nc.sync.dma_start(e_dup[t, h][:], e_win[t][:, h * HALF : (h + 1) * HALF])
 
         for t in range(PACK):
-            for h in range(2):
-                a, b = h * HALF, (h + 1) * HALF
-                tap_add(y_sum[:, t, a:b], y_win[t], y_dup[t], a, b)
+            for a, b in ((0, HALF), (HALF, S)) if t == 1 else ((0, S),):
+                tap_add(y_sum[:, t, a:b], y_win[t], y_dup[t][:, a:b], a, b)
             nc.scalar.activation(gate[:, t, :], y_sum[:, t, :], SIGMOID)
 
         oq = sb("oq", [P, S], U32)
@@ -179,18 +183,19 @@ def tile_picked_glutap_none_po_kernel(
 
         def gather_e(c, t):
             a, b = CHUNKS[c]
-            tap_add(e_sum[c][:, t, :], e_win[t], e_dup[t], a, b)
+            h = a // HALF
+            tap_add(e_sum[c][:, t, :], e_win[t], e_dup[t, h][:, a - h * HALF : b - h * HALF], a, b)
 
         def gated(c):
             a, b = CHUNKS[c]
             nc.vector.tensor_tensor(
-                z_bf[c][:].rearrange("p (c i) t -> p c t i", i=4),
-                e_sum[c].rearrange("p t (c i) -> p c t i", i=4),
-                gate[:, :, a:b].rearrange("p t (c i) -> p c t i", i=4),
+                z_bf[c][:].rearrange("p (c i) t -> p c t i", i=2),
+                e_sum[c].rearrange("p t (c i) -> p c t i", i=2),
+                gate[:, :, a:b].rearrange("p t (c i) -> p c t i", i=2),
                 MULT,
             )
 
-        def last_layer(c):
+        def last_layer(c, w3q, w3s):
             a, b = CHUNKS[c]
             nc.vector.quantize_mx(
                 out=zq[c][:].bitcast(FP8X4), scales=zs[c][:], in_=z_bf[c][:].rearrange("p n t -> p (n t)")
@@ -211,33 +216,33 @@ def tile_picked_glutap_none_po_kernel(
                 nc.scalar.copy(o_bf[u][:], bank[:].rearrange("p t n -> p n t"))
                 o_f32 = sb(f"o_f32{u}", [P, PACK, UNIT], F32)
                 nc.scalar.copy(o_f32[:], bank[:])
-                nc.sync.dma_start(out_rows[:, :, n0 : n0 + UNIT], o_f32[:])
+                queue = nc.scalar if n0 + UNIT == S else nc.sync
+                queue.dma_start(out_rows[:, :, n0 : n0 + UNIT], o_f32[:])
 
         def hand_on(u):
             a, b = u * UNIT, (u + 1) * UNIT
             nc.vector.quantize_mx(
                 out=oq[:, a:b].bitcast(FP8X4), scales=osc[:, a:b], in_=o_bf[u][:].rearrange("p n t -> p (n t)")
             )
-            nc.sync.dma_start(out_words[:, a:b], oq[:, a:b].bitcast(I32))
 
         for t in range(1, PACK):
             gather_e(0, t)
+        w3q = deal("e_dup2_0", w3_raw, U32)
         gated(0)
-        gather_e(1, 1)
-        last_layer(0)
-        gather_e(1, 2)
-        gather_e(1, 3)
+        w3s = deal("e_dup3_0", w3s_raw, U8)
+        last_layer(0, w3q, w3s)
+        for t in range(1, PACK):
+            gather_e(1, t)
         gated(1)
-        gather_e(2, 1)
-        last_layer(1)
-        gather_e(2, 2)
-        hand_on(0)
-        gather_e(2, 3)
+        last_layer(1, w3q, w3s)
+        for t in range(1, PACK):
+            gather_e(2, t)
         gated(2)
-        hand_on(1)
-        last_layer(2)
-        hand_on(2)
-        hand_on(3)
+        last_layer(2, w3q, w3s)
+        for u in range(S // UNIT):
+            hand_on(u)
+        for a, b in ((0, S - UNIT), (S - UNIT, S)):
+            nc.sync.dma_start(out_words[:, a:b], oq[:, a:b].bitcast(I32))
         for q in range(4):
-            queue = nc.scalar if q % 2 else nc.sync
+            queue = nc.scalar if q >= 2 else nc.sync
             queue.dma_start(out_2[0, 4 * q : 4 * q + 4, :].bitcast(I32), osc[32 * q : 32 * q + 4, :].bitcast(I32))

@@ -20,6 +20,7 @@ HALF = S // 2
 UNIT = 128
 FLOPS = 3 * 2 * 512 * 512 * 512
 CHUNKS = ((0, 256), (256, 384), (384, 512))
+M_SCALAR = 88
 
 
 def tile_picked_glutap_none_po_kernel(
@@ -37,8 +38,8 @@ def tile_picked_glutap_none_po_kernel(
             return dram[0].rearrange("p n t -> p (n t)").bitcast(I32)
 
         def load_scale_rows(queue, plane, dram):
-            for q in range(4):
-                queue.dma_start(plane[32 * q : 32 * q + 4, :].bitcast(I32), dram[0, 4 * q : 4 * q + 4, :].bitcast(I32))
+            for r in range(4):
+                queue.dma_start(plane[r:P:32, :].bitcast(I32), dram[0, r:16:4, :].bitcast(I32))
 
         def entries(lists, a, b):
             return lists[:, a // 16 : b // 16]
@@ -51,7 +52,7 @@ def tile_picked_glutap_none_po_kernel(
         w3_raw = sb("w3_raw", [P, H], U32)
         w1s_raw = sb("w1s_raw", [P, H], U8)
         w3s_raw = sb("w3s_raw", [P, H], U8)
-        w2_raw = [sb(f"w2_raw{h}", [P, PACK, HALF], F32) for h in range(2)]
+        w2_raw = sb("w2_raw", [P, PACK, H], F32)
         warm = sb("warm", [P, 16], F32)
         warm_out = sb("warm_out", [P, 16], F32)
 
@@ -61,10 +62,9 @@ def tile_picked_glutap_none_po_kernel(
         nc.vector.memset(w3s_raw[:].bitcast(I32), 0)
 
         w2_rows = w2.rearrange("(p j) c -> p j c", j=PACK)
-        nc.sync.dma_start(w2_raw[0][:], w2_rows[:, :, 0:HALF])
+        nc.sync.dma_start(w2_raw[:], w2_rows)
         nc.sync.dma_start(offs_sb[:], offs)
         load_scale_rows(nc.sync, xs_tab, x_scales)
-        nc.sync.dma_start(w2_raw[1][:], w2_rows[:, :, HALF:H])
         nc.sync.dma_start(x_tab[:].bitcast(I32), words_view(x_words))
         nc.sync.dma_start(w1_raw[:].bitcast(I32), words_view(w1_words))
         load_scale_rows(nc.sync, w1s_raw, w1_scales)
@@ -77,10 +77,10 @@ def tile_picked_glutap_none_po_kernel(
         nc.vector.tensor_copy(xs[:], xs_tab[:].indirect(offs_sb[:]))
 
         w2_bf = sb("w2_bf", [P, PACK, P, PACK], BF16)
-        for h in range(2):
-            dst = w2_bf[:, :, 64 * h : 64 * h + 64, :].rearrange("p t m j -> p m t j")
-            src = w2_raw[h][:].rearrange("p j (m t) -> p m t j", t=PACK)
-            if h == 0:
+        for m0, m1 in ((0, M_SCALAR), (M_SCALAR, P)):
+            dst = w2_bf[:, :, m0:m1, :].rearrange("p t m j -> p m t j")
+            src = w2_raw[:, :, PACK * m0 : PACK * m1].rearrange("p j (m t) -> p m t j", t=PACK)
+            if m0 == 0:
                 nc.scalar.copy(dst, src)
             else:
                 nc.vector.tensor_copy(dst, src)
@@ -96,7 +96,7 @@ def tile_picked_glutap_none_po_kernel(
             return dealt
 
         w2q = sb("w2q", [P, PACK, P], U32)
-        w2s = sb("w2s", [P, PACK, P], U8)
+        w2s = sb("xs_tab", [P, PACK, P], U8)
         nc.vector.quantize_mx(
             out=w2q[:].rearrange("p t m -> p (t m)").bitcast(FP8X4),
             scales=w2s[:].rearrange("p t m -> p (t m)"),
@@ -124,28 +124,30 @@ def tile_picked_glutap_none_po_kernel(
         e_win = [sb(f"e_win{t}", [P, S], F32) for t in range(PACK)]
         y_sum = sb("y_sum", [P, PACK, S], F32)
         gate = sb("gate", [P, PACK, S], F32)
-        e_ring = sb("e_ring", [P, 1 + PACK, HALF], F32)
-        e_sum = [e_ring[:, 1 : 1 + PACK, :], e_ring[:, 0:PACK, 0:UNIT], e_ring[:, 0:PACK, UNIT:HALF]]
+        e_ring = sb("e_ring", [P, 2 + PACK, HALF], F32)
+        e_sum = [e_ring[:, 2 : 2 + PACK, :], e_ring[:, 0:PACK, 0:UNIT], e_ring[:, 0:PACK, UNIT:HALF]]
 
         def tap_add(dst, win, plain, a, b):
             nc.vector.tensor_tensor(dst, win[:].indirect(entries(tap_sb, a, b)), plain, ADD)
 
-        y_win = {t: sb(f"y_win{t}", [P, 2 * S], F32) for t in (0, 2, 3)}
-        e0_dup = y_win[0][:, S : 2 * S]
+        y_win = [sb(f"y_win{t}", [P, 2 * S if t else S], F32) for t in range(PACK)]
+        e0_dup1 = sb("e0_dup1", [P, HALF], F32)
+        e0_dup = [y_win[1][:, S : S + HALF], e0_dup1[:]]
         for h in range(2):
             a, b = h * HALF, (h + 1) * HALF
             bank = project(w2q, w2s, 0, a, b, h)
             nc.scalar.copy(e_win[0][:, a:b], bank[:, 0:HALF])
-            nc.scalar.copy(e0_dup[:, a:b], bank[:, 0:HALF])
+            nc.scalar.copy(e0_dup[h], bank[:, 0:HALF])
 
         w1q = deal("w1q", w1_raw, U32)
         w1s = deal("w1s", w1s_raw, U8)
+        w3q = deal("w3q", w3_raw, U32)
+        w3s = deal("w3s", w3s_raw, U8)
 
         for h in range(2):
             a, b = h * HALF, (h + 1) * HALF
-            tap_add(e_ring[:, 1 - h, :], e_win[0], e0_dup[:, a:b], a, b)
+            tap_add(e_ring[:, 2 - 2 * h, :], e_win[0], e0_dup[h], a, b)
 
-        y_win[1] = sb("e_win0", [P, 2 * S], F32)
         y3_dup = sb("y3_dup", [P, S], F32)
         y_dup = [y_win[t + 1][:, S : 2 * S] for t in range(PACK - 1)] + [y3_dup[:]]
         y_bank = {}
@@ -163,61 +165,84 @@ def tile_picked_glutap_none_po_kernel(
         for t in range(1, PACK):
             bank = project(w2q, w2s, t, 0, S, 1 + t)
             nc.scalar.copy(e_win[t][:], bank[:])
-            for h in range(2):
-                e_dup[t, h] = sb(f"e_dup{t}_{h}", [P, HALF], F32)
-                nc.sync.dma_start(e_dup[t, h][:], e_win[t][:, h * HALF : (h + 1) * HALF])
+            e_dup[t, 0] = sb(f"e_dup{t}", [P, HALF], F32)
+            nc.sync.dma_start(e_dup[t, 0][:], e_win[t][:, 0:HALF])
 
         for t in range(PACK):
-            for a, b in ((0, HALF), (HALF, S)) if t == 1 else ((0, S),):
+            for a, b in ((0, HALF), (HALF, S)) if t < 2 else ((0, S),):
                 tap_add(y_sum[:, t, a:b], y_win[t], y_dup[t][:, a:b], a, b)
             nc.scalar.activation(gate[:, t, :], y_sum[:, t, :], SIGMOID)
+
+        late = sb("y_win3", [P, PACK - 1, HALF], F32)
+        for t in range(1, PACK):
+            e_dup[t, 1] = late[:, t - 1, :]
+            nc.sync.dma_start(e_dup[t, 1], e_win[t][:, HALF:S])
 
         oq = sb("oq", [P, S], U32)
         osc = sb("osc", [P, S], U8)
         out_rows = out_0.rearrange("(p t) n -> p t n", t=PACK)
         out_words = words_view(out_1)
-        z_bf = [sb(f"z_bf{c}", [P, b - a, PACK], BF16) for c, (a, b) in enumerate(CHUNKS)]
-        zq = [sb(f"zq{c}", [P, b - a], U32) for c, (a, b) in enumerate(CHUNKS)]
-        zs = [sb(f"zs{c}", [P, b - a], U8) for c, (a, b) in enumerate(CHUNKS)]
-        o_bf = [sb(f"o_bf{u}", [P, UNIT, PACK], BF16) for u in range(S // UNIT)]
+        units = range(S // UNIT)
+        z_bf = [sb(f"z_bf{u}", [P, UNIT, PACK], BF16) for u in units]
+        zq = [sb(f"zq{u}", [P, UNIT], U32) for u in units]
+        zs = [sb(f"zs{u}", [P, UNIT], U8) for u in units]
+        o_bf = [sb(f"o_bf{u}", [P, UNIT, PACK], BF16) for u in units]
+        o_f32 = [sb(f"o_f32{u}", [P, PACK, UNIT], F32) for u in units]
+        o_bank = {}
 
         def gather_e(c, t):
             a, b = CHUNKS[c]
             h = a // HALF
             tap_add(e_sum[c][:, t, :], e_win[t], e_dup[t, h][:, a - h * HALF : b - h * HALF], a, b)
 
-        def gated(c):
-            a, b = CHUNKS[c]
+        def gated(c, u):
+            a = u * UNIT
+            off = a - CHUNKS[c][0]
             nc.vector.tensor_tensor(
-                z_bf[c][:].rearrange("p (c i) t -> p c t i", i=2),
-                e_sum[c].rearrange("p t (c i) -> p c t i", i=2),
-                gate[:, :, a:b].rearrange("p t (c i) -> p c t i", i=2),
+                z_bf[u][:].rearrange("p (c i) t -> p c t i", i=4),
+                e_sum[c][:, :, off : off + UNIT].rearrange("p t (c i) -> p c t i", i=4),
+                gate[:, :, a : a + UNIT].rearrange("p t (c i) -> p c t i", i=4),
                 MULT,
             )
-
-        def last_layer(c, w3q, w3s):
-            a, b = CHUNKS[c]
             nc.vector.quantize_mx(
-                out=zq[c][:].bitcast(FP8X4), scales=zs[c][:], in_=z_bf[c][:].rearrange("p n t -> p (n t)")
+                out=zq[u][:].bitcast(FP8X4), scales=zs[u][:], in_=z_bf[u][:].rearrange("p n t -> p (n t)")
             )
-            for n0 in range(a, b, UNIT):
-                u = n0 // UNIT
-                bank = psum.tile([P, PACK, UNIT], F32, name=f"bank{(6 + u) % 8}")
-                for t in range(PACK):
-                    nc.tensor.matmul_mx(
-                        bank[:, t, :],
-                        lhsT=w3q[:, t, :].bitcast(FP8X4),
-                        lhsT_scale=w3s[:, t, :],
-                        rhs=zq[c][:, n0 - a : n0 - a + UNIT].bitcast(FP8X4),
-                        rhs_scale=zs[c][:, n0 - a : n0 - a + UNIT],
-                        start=True,
-                        stop=True,
-                    )
-                nc.scalar.copy(o_bf[u][:], bank[:].rearrange("p t n -> p n t"))
-                o_f32 = sb(f"o_f32{u}", [P, PACK, UNIT], F32)
-                nc.scalar.copy(o_f32[:], bank[:])
-                queue = nc.scalar if n0 + UNIT == S else nc.sync
-                queue.dma_start(out_rows[:, :, n0 : n0 + UNIT], o_f32[:])
+
+        def product(dst, t, u):
+            nc.tensor.matmul_mx(
+                dst,
+                lhsT=w3q[:, t, :].bitcast(FP8X4),
+                lhsT_scale=w3s[:, t, :],
+                rhs=zq[u][:].bitcast(FP8X4),
+                rhs_scale=zs[u][:],
+                start=True,
+                stop=True,
+            )
+
+        def store_f32(u):
+            nc.sync.dma_start(out_rows[:, :, u * UNIT : (u + 1) * UNIT], o_f32[u][:])
+
+        def last_layer(u):
+            o_bank[u] = psum.tile([P, PACK, UNIT], F32, name=f"bank{(6 + u) % 8}")
+            for t in range(PACK):
+                product(o_bank[u][:, t, :], t, u)
+            nc.scalar.copy(o_bf[u][:], o_bank[u][:].rearrange("p t n -> p n t"))
+
+        def empty_bank(u):
+            nc.scalar.copy(o_f32[u][:], o_bank[u][:])
+            store_f32(u)
+
+        def last_layer_in_two_banks(u):
+            for k, copy in enumerate((nc.scalar.copy, nc.vector.tensor_copy)):
+                bank = psum.tile([P, 2, UNIT], F32, name=f"bank{1 + k}")
+                for t in range(2):
+                    product(bank[:, t, :], 2 * k + t, u)
+                copy(o_f32[u][:, 2 * k : 2 * k + 2, :], bank[:])
+            store_f32(u)
+            nc.vector.tensor_copy(
+                o_bf[u][:].rearrange("p (c i) t -> p c t i", i=4),
+                o_f32[u][:].rearrange("p t (c i) -> p c t i", i=4),
+            )
 
         def hand_on(u):
             a, b = u * UNIT, (u + 1) * UNIT
@@ -227,22 +252,24 @@ def tile_picked_glutap_none_po_kernel(
 
         for t in range(1, PACK):
             gather_e(0, t)
-        w3q = deal("e_dup2_0", w3_raw, U32)
-        gated(0)
-        w3s = deal("e_dup3_0", w3s_raw, U8)
-        last_layer(0, w3q, w3s)
+        for u in (0, 1):
+            gated(0, u)
+            last_layer(u)
+        for u in (0, 1):
+            empty_bank(u)
         for t in range(1, PACK):
             gather_e(1, t)
-        gated(1)
-        last_layer(1, w3q, w3s)
+        gated(1, 2)
+        last_layer(2)
         for t in range(1, PACK):
             gather_e(2, t)
-        gated(2)
-        last_layer(2, w3q, w3s)
+        gated(2, 3)
+        last_layer_in_two_banks(3)
+        empty_bank(2)
         for u in range(S // UNIT):
             hand_on(u)
-        for a, b in ((0, S - UNIT), (S - UNIT, S)):
+        for a, b in ((0, HALF), (HALF, S)):
             nc.sync.dma_start(out_words[:, a:b], oq[:, a:b].bitcast(I32))
         for q in range(4):
             queue = nc.scalar if q >= 2 else nc.sync
-            queue.dma_start(out_2[0, 4 * q : 4 * q + 4, :].bitcast(I32), osc[32 * q : 32 * q + 4, :].bitcast(I32))
+            queue.dma_start(out_2[0, q:16:4, :].bitcast(I32), osc[q:P:32, :].bitcast(I32))

@@ -1,6 +1,7 @@
 from contextlib import ExitStack
 
 import concourse.mybir as mybir
+from concourse.masks import make_identity
 
 F32 = mybir.dt.float32
 BF16 = mybir.dt.bfloat16
@@ -20,7 +21,6 @@ HALF = S // 2
 UNIT = 128
 FLOPS = 3 * 2 * 512 * 512 * 512
 CHUNKS = ((0, 256), (256, 384), (384, 512))
-M_SCALAR = 88
 
 
 def tile_picked_glutap_none_po_kernel(
@@ -29,10 +29,14 @@ def tile_picked_glutap_none_po_kernel(
     nc = tc.nc
     with ExitStack() as ctx:
         keep = ctx.enter_context(tc.tile_pool(name="keep", bufs=1))
+        turns = ctx.enter_context(tc.tile_pool(name="turns", bufs=1))
         psum = ctx.enter_context(tc.psum_pool(name="psum", bufs=1))
 
         def sb(name, shape, dtype):
             return keep.tile(shape, dtype, name=name, align_bytes=64)
+
+        def bank(k, shape):
+            return psum.tile(shape, F32, name=f"bank{k}")
 
         def words_view(dram):
             return dram[0].rearrange("p n t -> p (n t)").bitcast(I32)
@@ -48,42 +52,34 @@ def tile_picked_glutap_none_po_kernel(
         tap_sb = keep.tile([P, S // 16], U16, name="tap_sb")
         x_tab = sb("x_tab", [P, T], U32)
         xs_tab = sb("xs_tab", [P, T], U8)
+        w1s = sb("w1s", [P, PACK, P], U8)
+        xs = sb("xs", [P, S], U8)
         w1_raw = sb("w1_raw", [P, H], U32)
         w3_raw = sb("w3_raw", [P, H], U32)
         w1s_raw = sb("w1s_raw", [P, H], U8)
         w3s_raw = sb("w3s_raw", [P, H], U8)
-        w2_raw = sb("w2_raw", [P, PACK, H], F32)
-        warm = sb("warm", [P, 16], F32)
+        w2_raw = [
+            sb("w2_raw0", [P, PACK, H // 2], F32),
+            turns.tile([P, PACK, H // 2], F32, name="w2_raw1", offset=4 * S),
+        ]
         warm_out = sb("warm_out", [P, 16], F32)
+        ident = sb("ident", [P, P], F32)
 
         nc.vector.memset(xs_tab[:].bitcast(I32), 0)
-        nc.vector.memset(warm[:], 0.0)
-        nc.vector.memset(w1s_raw[:].bitcast(I32), 0)
-        nc.vector.memset(w3s_raw[:].bitcast(I32), 0)
+        nc.gpsimd.memset(w1s_raw[:].bitcast(I32), 0)
+        nc.gpsimd.memset(w1s[:].rearrange("p t m -> p (t m)").bitcast(I32), 0)
+        nc.gpsimd.memset(w3s_raw[:].bitcast(I32), 0)
+        make_identity(nc, ident[:])
 
         w2_rows = w2.rearrange("(p j) c -> p j c", j=PACK)
-        nc.sync.dma_start(w2_raw[:], w2_rows)
-        nc.sync.dma_start(offs_sb[:], offs)
-        load_scale_rows(nc.sync, xs_tab, x_scales)
-        nc.sync.dma_start(x_tab[:].bitcast(I32), words_view(x_words))
         nc.sync.dma_start(w1_raw[:].bitcast(I32), words_view(w1_words))
-        load_scale_rows(nc.sync, w1s_raw, w1_scales)
-        nc.sync.dma_start(w3_raw[:].bitcast(I32), words_view(w3_words))
-        nc.sync.dma_start(tap_sb[:], tap)
-        load_scale_rows(nc.sync, w3s_raw, w3_scales)
-        nc.scalar.activation(warm_out[:], warm[:], SIGMOID)
-
-        xs = sb("xs", [P, S], U8)
-        nc.vector.tensor_copy(xs[:], xs_tab[:].indirect(offs_sb[:]))
-
-        w2_bf = sb("w2_bf", [P, PACK, P, PACK], BF16)
-        for m0, m1 in ((0, M_SCALAR), (M_SCALAR, P)):
-            dst = w2_bf[:, :, m0:m1, :].rearrange("p t m j -> p m t j")
-            src = w2_raw[:, :, PACK * m0 : PACK * m1].rearrange("p j (m t) -> p m t j", t=PACK)
-            if m0 == 0:
-                nc.scalar.copy(dst, src)
-            else:
-                nc.vector.tensor_copy(dst, src)
+        nc.sync.dma_start(offs_sb[:], offs)
+        nc.scalar.dma_start(w1s_raw[0:P:8, :].bitcast(I32), w1_scales[0].bitcast(I32))
+        for r in range(4):
+            queue = nc.sync if r < 2 else nc.scalar
+            queue.dma_start(xs_tab[r:P:32, :].bitcast(I32), x_scales[0, r:16:4, :].bitcast(I32))
+        nc.sync.dma_start(x_tab[:].bitcast(I32), words_view(x_words))
+        nc.scalar.activation(warm_out[:], ident[:, 0:16], SIGMOID)
 
         def deal(name, raw, dtype):
             dealt = sb(name, [P, PACK, P], dtype)
@@ -95,13 +91,19 @@ def tile_picked_glutap_none_po_kernel(
                 )
             return dealt
 
-        w2q = sb("w2q", [P, PACK, P], U32)
-        w2s = sb("xs_tab", [P, PACK, P], U8)
-        nc.vector.quantize_mx(
-            out=w2q[:].rearrange("p t m -> p (t m)").bitcast(FP8X4),
-            scales=w2s[:].rearrange("p t m -> p (t m)"),
-            in_=w2_bf[:].rearrange("p t m j -> p (t m j)"),
-        )
+        w1s_rows = deal("w1s_rows", w1s_raw, U8)
+        w1q = deal("w1q", w1_raw, U32)
+        nc.vector.tensor_copy(xs[:], xs_tab[:].indirect(offs_sb[:]))
+        for r in range(4):
+            nc.sync.dma_start(
+                w1s[r:P:32].rearrange("p t m -> p (t m)").bitcast(I32),
+                w1s_rows[8 * r : P : 32].rearrange("p t m -> p (t m)").bitcast(I32),
+            )
+        nc.sync.dma_start(w2_raw[0][:], w2_rows[:, :, 0 : H // 2])
+        nc.sync.dma_start(tap_sb[:], tap)
+        nc.sync.dma_start(w2_raw[1][:], w2_rows[:, :, H // 2 : H])
+        nc.sync.dma_start(w3_raw[:].bitcast(I32), words_view(w3_words))
+        load_scale_rows(nc.sync, w3s_raw, w3_scales)
 
         xq = sb("xq", [P, S], U32)
         for h in range(2):
@@ -109,9 +111,9 @@ def tile_picked_glutap_none_po_kernel(
             nc.vector.tensor_copy(xq[:, a:b], x_tab[:].indirect(entries(offs_sb, a, b)))
 
         def project(wq, ws, t, a, b, k):
-            bank = psum.tile([P, S], F32, name=f"bank{k}")
+            acc = bank(k, [P, S])
             nc.tensor.matmul_mx(
-                bank[:, 0 : b - a],
+                acc[:, 0 : b - a],
                 lhsT=wq[:, t, :].bitcast(FP8X4),
                 lhsT_scale=ws[:, t, :],
                 rhs=xq[:, a:b].bitcast(FP8X4),
@@ -119,64 +121,104 @@ def tile_picked_glutap_none_po_kernel(
                 start=True,
                 stop=True,
             )
-            return bank
+            return acc
+
+        w2_bf = sb("w2_bf", [P, PACK, P, PACK], BF16)
+
+        def round_w2(h, copy):
+            m0, m1 = h * P // 2, (h + 1) * P // 2
+            copy(
+                w2_bf[:, :, m0:m1, :].rearrange("p t m j -> p m t j"),
+                w2_raw[h][:].rearrange("p j (m t) -> p m t j", t=PACK),
+            )
+
+        y_win = {}
+        for t in range(2):
+            y_win[t] = sb(f"y_win{t}", [P, 2 * S], F32)
+        for h in range(2):
+            a, b = h * HALF, (h + 1) * HALF
+            acc = project(w1q, w1s, 0, a, b, h)
+            nc.scalar.copy(y_win[0][:, a:b], acc[:, 0:HALF])
+        y_acc = {t: project(w1q, w1s, t, 0, S, 1 + t) for t in range(1, PACK)}
+        nc.scalar.copy(y_win[1][:, 0:S], y_acc[1][:])
+        round_w2(0, nc.vector.tensor_copy)
+        round_w2(1, nc.scalar.copy)
+        for t in (2, 3):
+            y_win[t] = turns.tile([P, 2 * S], F32, name=f"y_win{t}", offset=8 * S * (t - 2))
+            nc.scalar.copy(y_win[t][:, 0:S], y_acc[t][:])
+
+        y_tap = {}
+        sum_bank = {}
+        gate = {}
+
+        def gather_y(t, name):
+            y_tap[t] = sb(name, [P, S], F32)
+            nc.vector.tensor_copy(y_tap[t][:], y_win[t][:].indirect(tap_sb[:]))
+
+        def add_turned(t, k):
+            sum_bank[t] = bank(k, [P, S])
+            for u in range(PACK):
+                cols = slice(u * UNIT, (u + 1) * UNIT)
+                nc.tensor.matmul(
+                    sum_bank[t][:, cols], y_win[t][:, cols], ident[:], start=(u == 0), stop=False, is_transpose=True
+                )
+            for u in range(PACK):
+                cols = slice(u * UNIT, (u + 1) * UNIT)
+                nc.tensor.matmul(
+                    sum_bank[t][:, cols], y_tap[t][:, cols], ident[:], start=False, stop=(u == PACK - 1), is_transpose=True
+                )
+
+        def squash(t):
+            nc.scalar.activation(y_win[t][:, S : 2 * S], sum_bank[t][:], SIGMOID)
+
+        def gate_back(t, u):
+            if t == 0:
+                gate[u] = bank((5 + u) % 8, [P, PACK, UNIT])
+            nc.tensor.transpose(gate[u][:, t, :], y_win[t][:, S + u * UNIT : S + (u + 1) * UNIT], ident[:])
+
+        gather_y(0, "w2_raw0")
+        gather_y(1, "y_tap1")
+
+        w2q = sb("w2q", [P, PACK, P], U32)
+        w2s = sb("w2s", [P, PACK, P], U8)
+        nc.vector.quantize_mx(
+            out=w2q[:].rearrange("p t m -> p (t m)").bitcast(FP8X4),
+            scales=w2s[:].rearrange("p t m -> p (t m)"),
+            in_=w2_bf[:].rearrange("p t m j -> p (t m j)"),
+        )
+        gather_y(2, "y_tap2")
+        gather_y(3, "y_tap3")
+        w3q = sb("w2_bf", [P, PACK, P], U32)
+        w3s = sb("w3s", [P, PACK, P], U8)
+        for dealt, raw in ((w3q, w3_raw), (w3s, w3s_raw)):
+            nc.gpsimd.tensor_copy(dealt[:], raw[:].rearrange("p (m t) -> p t m", t=PACK))
 
         e_win = [sb(f"e_win{t}", [P, S], F32) for t in range(PACK)]
-        y_sum = sb("y_sum", [P, PACK, S], F32)
-        gate = sb("gate", [P, PACK, S], F32)
+        e_dup = [sb(f"e_dup{t}", [P, S], F32) for t in range(PACK)]
+        e_acc = {}
+
+        def empty_e(t):
+            nc.scalar.copy(e_win[t][:], e_acc[t][:])
+            nc.scalar.copy(e_dup[t][:, 0:HALF], e_acc[t][:, 0:HALF])
+            nc.sync.dma_start(e_dup[t][:, HALF:S], e_win[t][:, HALF:S])
+
+        for t in (0, 1):
+            add_turned(t, 5 + t)
+        squash(0)
+        for t in range(PACK):
+            e_acc[t] = project(w2q, w2s, t, 0, S, 1 + t)
+        for t in range(PACK):
+            empty_e(t)
+        squash(1)
+        for t in (2, 3):
+            add_turned(t, (5 + t) % 8)
+            squash(t)
+        for u in range(PACK):
+            for t in range(PACK):
+                gate_back(t, u)
+
         e_ring = sb("e_ring", [P, 2 + PACK, HALF], F32)
         e_sum = [e_ring[:, 2 : 2 + PACK, :], e_ring[:, 0:PACK, 0:UNIT], e_ring[:, 0:PACK, UNIT:HALF]]
-
-        def tap_add(dst, win, plain, a, b):
-            nc.vector.tensor_tensor(dst, win[:].indirect(entries(tap_sb, a, b)), plain, ADD)
-
-        y_win = [sb(f"y_win{t}", [P, 2 * S if t else S], F32) for t in range(PACK)]
-        e0_dup1 = sb("e0_dup1", [P, HALF], F32)
-        e0_dup = [y_win[1][:, S : S + HALF], e0_dup1[:]]
-        for h in range(2):
-            a, b = h * HALF, (h + 1) * HALF
-            bank = project(w2q, w2s, 0, a, b, h)
-            nc.scalar.copy(e_win[0][:, a:b], bank[:, 0:HALF])
-            nc.scalar.copy(e0_dup[h], bank[:, 0:HALF])
-
-        w1q = deal("w1q", w1_raw, U32)
-        w1s = deal("w1s", w1s_raw, U8)
-        w3q = deal("w3q", w3_raw, U32)
-        w3s = deal("w3s", w3s_raw, U8)
-
-        for h in range(2):
-            a, b = h * HALF, (h + 1) * HALF
-            tap_add(e_ring[:, 2 - 2 * h, :], e_win[0], e0_dup[h], a, b)
-
-        y3_dup = sb("y3_dup", [P, S], F32)
-        y_dup = [y_win[t + 1][:, S : 2 * S] for t in range(PACK - 1)] + [y3_dup[:]]
-        y_bank = {}
-        for k, t in enumerate((0, 2, 1, 3)):
-            y_bank[t] = project(w1q, w1s, t, 0, S, 2 + k)
-            nc.scalar.copy(y_win[t][:, 0:S], y_bank[t][:])
-            if t == 0:
-                nc.vector.tensor_copy(y_dup[t], y_win[t][:, 0:S])
-            elif t != 1:
-                nc.sync.dma_start(y_dup[t], y_win[t][:, 0:S])
-        for h in range(2):
-            a, b = h * HALF, (h + 1) * HALF
-            nc.scalar.copy(y_dup[1][:, a:b], y_bank[1][:, a:b])
-        e_dup = {}
-        for t in range(1, PACK):
-            bank = project(w2q, w2s, t, 0, S, 1 + t)
-            nc.scalar.copy(e_win[t][:], bank[:])
-            e_dup[t, 0] = sb(f"e_dup{t}", [P, HALF], F32)
-            nc.sync.dma_start(e_dup[t, 0][:], e_win[t][:, 0:HALF])
-
-        for t in range(PACK):
-            for a, b in ((0, HALF), (HALF, S)) if t < 2 else ((0, S),):
-                tap_add(y_sum[:, t, a:b], y_win[t], y_dup[t][:, a:b], a, b)
-            nc.scalar.activation(gate[:, t, :], y_sum[:, t, :], SIGMOID)
-
-        late = sb("y_win3", [P, PACK - 1, HALF], F32)
-        for t in range(1, PACK):
-            e_dup[t, 1] = late[:, t - 1, :]
-            nc.sync.dma_start(e_dup[t, 1], e_win[t][:, HALF:S])
 
         oq = sb("oq", [P, S], U32)
         osc = sb("osc", [P, S], U8)
@@ -186,22 +228,22 @@ def tile_picked_glutap_none_po_kernel(
         z_bf = [sb(f"z_bf{u}", [P, UNIT, PACK], BF16) for u in units]
         zq = [sb(f"zq{u}", [P, UNIT], U32) for u in units]
         zs = [sb(f"zs{u}", [P, UNIT], U8) for u in units]
-        o_bf = [sb(f"o_bf{u}", [P, UNIT, PACK], BF16) for u in units]
+        o_bf = {u: sb(f"o_bf{u}", [P, UNIT, PACK], BF16) for u in range(3)}
         o_f32 = [sb(f"o_f32{u}", [P, PACK, UNIT], F32) for u in units]
         o_bank = {}
 
         def gather_e(c, t):
             a, b = CHUNKS[c]
-            h = a // HALF
-            tap_add(e_sum[c][:, t, :], e_win[t], e_dup[t, h][:, a - h * HALF : b - h * HALF], a, b)
+            nc.vector.tensor_tensor(
+                e_sum[c][:, t, :], e_win[t][:].indirect(entries(tap_sb, a, b)), e_dup[t][:, a:b], ADD
+            )
 
         def gated(c, u):
-            a = u * UNIT
-            off = a - CHUNKS[c][0]
+            off = u * UNIT - CHUNKS[c][0]
             nc.vector.tensor_tensor(
                 z_bf[u][:].rearrange("p (c i) t -> p c t i", i=4),
                 e_sum[c][:, :, off : off + UNIT].rearrange("p t (c i) -> p c t i", i=4),
-                gate[:, :, a : a + UNIT].rearrange("p t (c i) -> p c t i", i=4),
+                gate[u][:].rearrange("p t (c i) -> p c t i", i=4),
                 MULT,
             )
             nc.vector.quantize_mx(
@@ -223,26 +265,26 @@ def tile_picked_glutap_none_po_kernel(
             nc.sync.dma_start(out_rows[:, :, u * UNIT : (u + 1) * UNIT], o_f32[u][:])
 
         def last_layer(u):
-            o_bank[u] = psum.tile([P, PACK, UNIT], F32, name=f"bank{(6 + u) % 8}")
+            o_bank[u] = bank(1 + u, [P, PACK, UNIT])
             for t in range(PACK):
                 product(o_bank[u][:, t, :], t, u)
-            nc.scalar.copy(o_bf[u][:], o_bank[u][:].rearrange("p t n -> p n t"))
-
-        def empty_bank(u):
             nc.scalar.copy(o_f32[u][:], o_bank[u][:])
             store_f32(u)
 
+        def empty_bank(u):
+            nc.scalar.copy(o_bf[u][:], o_bank[u][:].rearrange("p t n -> p n t"))
+
         def last_layer_in_two_banks(u):
-            for k, copy in enumerate((nc.scalar.copy, nc.vector.tensor_copy)):
-                bank = psum.tile([P, 2, UNIT], F32, name=f"bank{1 + k}")
-                for t in range(2):
-                    product(bank[:, t, :], 2 * k + t, u)
-                copy(o_f32[u][:, 2 * k : 2 * k + 2, :], bank[:])
-            store_f32(u)
+            acc = bank(4, [P, PACK, UNIT])
+            for t in range(PACK):
+                product(acc[:, t, :], t, u)
+            o_bf[u] = sb("o_bf1", [P, UNIT, PACK], BF16)
             nc.vector.tensor_copy(
                 o_bf[u][:].rearrange("p (c i) t -> p c t i", i=4),
-                o_f32[u][:].rearrange("p t (c i) -> p c t i", i=4),
+                acc[:].rearrange("p t (c i) -> p c t i", i=4),
             )
+            nc.scalar.copy(o_f32[u][:], acc[:])
+            nc.scalar.dma_start(out_rows[:, :, u * UNIT : (u + 1) * UNIT], o_f32[u][:])
 
         def hand_on(u):
             a, b = u * UNIT, (u + 1) * UNIT
@@ -250,26 +292,28 @@ def tile_picked_glutap_none_po_kernel(
                 out=oq[:, a:b].bitcast(FP8X4), scales=osc[:, a:b], in_=o_bf[u][:].rearrange("p n t -> p (n t)")
             )
 
-        for t in range(1, PACK):
+        for t in range(PACK):
             gather_e(0, t)
         for u in (0, 1):
             gated(0, u)
             last_layer(u)
         for u in (0, 1):
             empty_bank(u)
-        for t in range(1, PACK):
+        for t in range(PACK):
             gather_e(1, t)
         gated(1, 2)
         last_layer(2)
-        for t in range(1, PACK):
+        empty_bank(2)
+        for t in range(PACK):
             gather_e(2, t)
         gated(2, 3)
+        for u in range(2):
+            hand_on(u)
         last_layer_in_two_banks(3)
-        empty_bank(2)
-        for u in range(S // UNIT):
+        for u in range(2, 4):
             hand_on(u)
         for a, b in ((0, HALF), (HALF, S)):
             nc.sync.dma_start(out_words[:, a:b], oq[:, a:b].bitcast(I32))
         for q in range(4):
-            queue = nc.scalar if q >= 2 else nc.sync
+            queue = nc.scalar if q == 3 else nc.sync
             queue.dma_start(out_2[0, q:16:4, :].bitcast(I32), osc[q:P:32, :].bitcast(I32))

@@ -67,14 +67,12 @@ def tile_picked_glutap_none_po_kernel(
 
         nc.vector.memset(xs_tab[:].bitcast(I32), 0)
         nc.gpsimd.memset(w1s_raw[:].bitcast(I32), 0)
-        nc.gpsimd.memset(w1s[:].rearrange("p t m -> p (t m)").bitcast(I32), 0)
         nc.gpsimd.memset(w3s_raw[:].bitcast(I32), 0)
         make_identity(nc, ident[:])
 
         w2_rows = w2.rearrange("(p j) c -> p j c", j=PACK)
         nc.sync.dma_start(w1_raw[:].bitcast(I32), words_view(w1_words))
         nc.sync.dma_start(offs_sb[:], offs)
-        nc.scalar.dma_start(w1s_raw[0:P:8, :].bitcast(I32), w1_scales[0].bitcast(I32))
         for r in range(4):
             queue = nc.sync if r < 2 else nc.scalar
             queue.dma_start(xs_tab[r:P:32, :].bitcast(I32), x_scales[0, r:16:4, :].bitcast(I32))
@@ -91,14 +89,10 @@ def tile_picked_glutap_none_po_kernel(
                 )
             return dealt
 
-        w1s_rows = deal("w1s_rows", w1s_raw, U8)
         w1q = deal("w1q", w1_raw, U32)
         nc.vector.tensor_copy(xs[:], xs_tab[:].indirect(offs_sb[:]))
-        for r in range(4):
-            nc.sync.dma_start(
-                w1s[r:P:32].rearrange("p t m -> p (t m)").bitcast(I32),
-                w1s_rows[8 * r : P : 32].rearrange("p t m -> p (t m)").bitcast(I32),
-            )
+        load_scale_rows(nc.sync, w1s_raw, w1_scales)
+        nc.gpsimd.tensor_copy(w1s[:], w1s_raw[:].rearrange("p (m t) -> p t m", t=PACK))
         nc.sync.dma_start(w2_raw[0][:], w2_rows[:, :, 0 : H // 2])
         nc.sync.dma_start(tap_sb[:], tap)
         nc.sync.dma_start(w2_raw[1][:], w2_rows[:, :, H // 2 : H])
@@ -125,13 +119,14 @@ def tile_picked_glutap_none_po_kernel(
 
         w2_bf = sb("w2_bf", [P, PACK, P, PACK], BF16)
 
-        def round_w2(h, copy):
-            m0, m1 = h * P // 2, (h + 1) * P // 2
+        def round_w2(h, g0, g1, copy):
+            m0 = h * P // 2
             copy(
-                w2_bf[:, :, m0:m1, :].rearrange("p t m j -> p m t j"),
-                w2_raw[h][:].rearrange("p j (m t) -> p m t j", t=PACK),
+                w2_bf[:, :, m0 + g0 : m0 + g1, :].rearrange("p t m j -> p m t j"),
+                w2_raw[h][:, :, PACK * g0 : PACK * g1].rearrange("p j (m t) -> p m t j", t=PACK),
             )
 
+        round_w2(0, 0, 16, nc.scalar.copy)
         y_win = {}
         for t in range(2):
             y_win[t] = sb(f"y_win{t}", [P, 2 * S], F32)
@@ -141,8 +136,9 @@ def tile_picked_glutap_none_po_kernel(
             nc.scalar.copy(y_win[0][:, a:b], acc[:, 0:HALF])
         y_acc = {t: project(w1q, w1s, t, 0, S, 1 + t) for t in range(1, PACK)}
         nc.scalar.copy(y_win[1][:, 0:S], y_acc[1][:])
-        round_w2(0, nc.vector.tensor_copy)
-        round_w2(1, nc.scalar.copy)
+        round_w2(0, 16, 64, nc.vector.tensor_copy)
+        round_w2(1, 0, 32, nc.scalar.copy)
+        round_w2(1, 32, 64, nc.gpsimd.tensor_copy)
         for t in (2, 3):
             y_win[t] = turns.tile([P, 2 * S], F32, name=f"y_win{t}", offset=8 * S * (t - 2))
             nc.scalar.copy(y_win[t][:, 0:S], y_acc[t][:])
@@ -297,6 +293,17 @@ def tile_picked_glutap_none_po_kernel(
         for u in (0, 1):
             gated(0, u)
             last_layer(u)
+        spare = bank(5, [P, S])
+        for k in range(3):
+            nc.tensor.matmul_mx(
+                spare[:],
+                lhsT=zq[1][:].bitcast(FP8X4),
+                lhsT_scale=zs[1][:],
+                rhs=w3q[:].rearrange("p t m -> p (t m)").bitcast(FP8X4),
+                rhs_scale=w3s[:].rearrange("p t m -> p (t m)"),
+                start=True,
+                stop=True,
+            )
         for u in (0, 1):
             empty_bank(u)
         for t in range(PACK):

@@ -59,8 +59,8 @@ def tile_picked_glutap_none_po_kernel(
         w1s_raw = sb("w1s_raw", [P, H], U8)
         w3s_raw = sb("w3s_raw", [P, H], U8)
         w2_raw = [
-            sb("w2_raw0", [P, PACK, H // 2], F32),
-            turns.tile([P, PACK, H // 2], F32, name="w2_raw1", offset=4 * S),
+            sb("w2_raw0", [P, PACK, H // 2], F32)[:],
+            turns.tile([P, 6 * S], F32, name="w2_raw1", offset=0)[:, 0 : 2 * S].rearrange("p (j c) -> p j c", j=PACK),
         ]
         warm_out = sb("warm_out", [P, 16], F32)
         ident = sb("ident", [P, P], F32)
@@ -92,10 +92,12 @@ def tile_picked_glutap_none_po_kernel(
         w1q = deal("w1q", w1_raw, U32)
         nc.vector.tensor_copy(xs[:], xs_tab[:].indirect(offs_sb[:]))
         load_scale_rows(nc.sync, w1s_raw, w1_scales)
-        nc.gpsimd.tensor_copy(w1s[:], w1s_raw[:].rearrange("p (m t) -> p t m", t=PACK))
-        nc.sync.dma_start(w2_raw[0][:], w2_rows[:, :, 0 : H // 2])
+        w1s_slices = w1s_raw[:].rearrange("p (m t) -> p t m", t=PACK)
+        for t0, t1 in ((0, 1), (1, PACK)):
+            nc.gpsimd.tensor_copy(w1s[:, t0:t1, :], w1s_slices[:, t0:t1, :])
+        nc.sync.dma_start(w2_raw[0], w2_rows[:, :, 0 : H // 2])
         nc.sync.dma_start(tap_sb[:], tap)
-        nc.sync.dma_start(w2_raw[1][:], w2_rows[:, :, H // 2 : H])
+        nc.sync.dma_start(w2_raw[1], w2_rows[:, :, H // 2 : H])
         nc.sync.dma_start(w3_raw[:].bitcast(I32), words_view(w3_words))
         load_scale_rows(nc.sync, w3s_raw, w3_scales)
 
@@ -126,7 +128,6 @@ def tile_picked_glutap_none_po_kernel(
                 w2_raw[h][:, :, PACK * g0 : PACK * g1].rearrange("p j (m t) -> p m t j", t=PACK),
             )
 
-        round_w2(0, 0, 16, nc.scalar.copy)
         y_win = {}
         for t in range(2):
             y_win[t] = sb(f"y_win{t}", [P, 2 * S], F32)
@@ -136,7 +137,7 @@ def tile_picked_glutap_none_po_kernel(
             nc.scalar.copy(y_win[0][:, a:b], acc[:, 0:HALF])
         y_acc = {t: project(w1q, w1s, t, 0, S, 1 + t) for t in range(1, PACK)}
         nc.scalar.copy(y_win[1][:, 0:S], y_acc[1][:])
-        round_w2(0, 16, 64, nc.vector.tensor_copy)
+        round_w2(0, 0, 64, nc.vector.tensor_copy)
         round_w2(1, 0, 32, nc.scalar.copy)
         round_w2(1, 32, 64, nc.gpsimd.tensor_copy)
         for t in (2, 3):
@@ -164,15 +165,21 @@ def tile_picked_glutap_none_po_kernel(
                     sum_bank[t][:, cols], y_tap[t][:, cols], ident[:], start=False, stop=(u == PACK - 1), is_transpose=True
                 )
 
+        gate_turned = {}
+
         def squash(t):
-            nc.scalar.activation(y_win[t][:, S : 2 * S], sum_bank[t][:], SIGMOID)
+            if t < 2:
+                gate_turned[t] = turns.tile([P, S], F32, name=f"gate_turned{t}", offset=16 * S + 4 * S * t)[:]
+            else:
+                gate_turned[t] = y_win[t][:, S : 2 * S]
+            nc.scalar.activation(gate_turned[t], sum_bank[t][:], SIGMOID)
 
         def gate_back(t, u):
             if t == 0:
                 gate[u] = bank((5 + u) % 8, [P, PACK, UNIT])
-            nc.tensor.transpose(gate[u][:, t, :], y_win[t][:, S + u * UNIT : S + (u + 1) * UNIT], ident[:])
+            nc.tensor.transpose(gate[u][:, t, :], gate_turned[t][:, u * UNIT : (u + 1) * UNIT], ident[:])
 
-        gather_y(0, "w2_raw0")
+        gather_y(0, "y_tap0")
         gather_y(1, "y_tap1")
 
         w2q = sb("w2q", [P, PACK, P], U32)
@@ -200,12 +207,12 @@ def tile_picked_glutap_none_po_kernel(
 
         for t in (0, 1):
             add_turned(t, 5 + t)
-        squash(0)
+        for t in (0, 1):
+            squash(t)
         for t in range(PACK):
             e_acc[t] = project(w2q, w2s, t, 0, S, 1 + t)
         for t in range(PACK):
             empty_e(t)
-        squash(1)
         for t in (2, 3):
             add_turned(t, (5 + t) % 8)
             squash(t)

@@ -30,6 +30,7 @@ def tile_picked_glutap_none_po_kernel(
     with ExitStack() as ctx:
         keep = ctx.enter_context(tc.tile_pool(name="keep", bufs=1))
         turns = ctx.enter_context(tc.tile_pool(name="turns", bufs=1))
+        late = ctx.enter_context(tc.tile_pool(name="late", bufs=1))
         psum = ctx.enter_context(tc.psum_pool(name="psum", bufs=1))
 
         def sb(name, shape, dtype):
@@ -55,9 +56,9 @@ def tile_picked_glutap_none_po_kernel(
         w1s = sb("w1s", [P, PACK, P], U8)
         xs = sb("xs", [P, S], U8)
         w1_raw = sb("w1_raw", [P, H], U32)
-        w3_raw = sb("w3_raw", [P, H], U32)
+        w3_raw = late.tile([P, H], U32, name="w3_raw", offset=9 * H, align_bytes=64)
         w1s_raw = sb("w1s_raw", [P, H], U8)
-        w3s_raw = sb("w3s_raw", [P, H], U8)
+        w3s_raw = late.tile([P, H], U8, name="w3s_raw", offset=8 * H, align_bytes=64)
         w2_raw = [
             sb("w2_raw0", [P, PACK, H // 2], F32)[:],
             turns.tile([P, 6 * S], F32, name="w2_raw1", offset=0)[:, 0 : 2 * S].rearrange("p (j c) -> p j c", j=PACK),
@@ -119,7 +120,7 @@ def tile_picked_glutap_none_po_kernel(
             )
             return acc
 
-        w2_bf = sb("w2_bf", [P, PACK, P, PACK], BF16)
+        w2_bf = late.tile([P, PACK, P, PACK], BF16, name="w2_bf", offset=0, align_bytes=64)
 
         def round_w2(h, g0, g1, copy):
             m0 = h * P // 2
@@ -131,10 +132,9 @@ def tile_picked_glutap_none_po_kernel(
         y_win = {}
         for t in range(2):
             y_win[t] = sb(f"y_win{t}", [P, 2 * S], F32)
-        for h in range(2):
-            a, b = h * HALF, (h + 1) * HALF
-            acc = project(w1q, w1s, 0, a, b, h)
-            nc.scalar.copy(y_win[0][:, a:b], acc[:, 0:HALF])
+        for (a, b), k in zip(CHUNKS, (0, 1, 7)):
+            acc = project(w1q, w1s, 0, a, b, k)
+            nc.scalar.copy(y_win[0][:, a:b], acc[:, 0 : b - a])
         y_acc = {t: project(w1q, w1s, t, 0, S, 1 + t) for t in range(1, PACK)}
         nc.scalar.copy(y_win[1][:, 0:S], y_acc[1][:])
         round_w2(0, 0, 64, nc.vector.tensor_copy)
@@ -172,7 +172,9 @@ def tile_picked_glutap_none_po_kernel(
                 gate_turned[t] = turns.tile([P, S], F32, name=f"gate_turned{t}", offset=16 * S + 4 * S * t)[:]
             else:
                 gate_turned[t] = y_win[t][:, S : 2 * S]
-            nc.scalar.activation(gate_turned[t], sum_bank[t][:], SIGMOID)
+
+        def squash_columns(t, a, b):
+            nc.scalar.activation(gate_turned[t][:, a:b], sum_bank[t][:, a:b], SIGMOID)
 
         def gate_back(t, u):
             if t == 0:
@@ -191,24 +193,30 @@ def tile_picked_glutap_none_po_kernel(
         )
         gather_y(2, "y_tap2")
         gather_y(3, "y_tap3")
-        w3q = sb("w2_bf", [P, PACK, P], U32)
+        w3q = late.tile([P, PACK, P], U32, name="w3q", offset=4 * H + 64, align_bytes=64)
         w3s = sb("w3s", [P, PACK, P], U8)
-        for dealt, raw in ((w3q, w3_raw), (w3s, w3s_raw)):
+        for dealt, raw in ((w3s, w3s_raw), (w3q, w3_raw)):
             nc.gpsimd.tensor_copy(dealt[:], raw[:].rearrange("p (m t) -> p t m", t=PACK))
 
         e_win = [sb(f"e_win{t}", [P, S], F32) for t in range(PACK)]
-        e_dup = [sb(f"e_dup{t}", [P, S], F32) for t in range(PACK)]
+        e_ring = late.tile([P, 2 + PACK, HALF], F32, name="e_ring", offset=9 * H, align_bytes=64)
+        e_low = [e_ring[:, PACK, :], e_ring[:, PACK + 1, :]] + [sb(f"e_low{t}", [P, HALF], F32)[:] for t in (2, 3)]
+        e_high = [sb(f"e_high{t}", [P, HALF], F32)[:] for t in range(PACK)]
         e_acc = {}
 
         def empty_e(t):
             nc.scalar.copy(e_win[t][:], e_acc[t][:])
-            nc.scalar.copy(e_dup[t][:, 0:HALF], e_acc[t][:, 0:HALF])
-            nc.sync.dma_start(e_dup[t][:, HALF:S], e_win[t][:, HALF:S])
+            if t < 2:
+                nc.gpsimd.tensor_copy(e_low[t], e_win[t][:, 0:HALF])
+            else:
+                nc.scalar.copy(e_low[t], e_acc[t][:, 0:HALF])
+            nc.sync.dma_start(e_high[t], e_win[t][:, HALF:S])
 
         for t in (0, 1):
             add_turned(t, 5 + t)
         for t in (0, 1):
             squash(t)
+            squash_columns(t, 0, S)
         for t in range(PACK):
             e_acc[t] = project(w2q, w2s, t, 0, S, 1 + t)
         for t in range(PACK):
@@ -216,12 +224,14 @@ def tile_picked_glutap_none_po_kernel(
         for t in (2, 3):
             add_turned(t, (5 + t) % 8)
             squash(t)
+        for a, b in ((0, HALF), (HALF, S)):
+            for t in (2, 3):
+                squash_columns(t, a, b)
         for u in range(PACK):
             for t in range(PACK):
                 gate_back(t, u)
 
-        e_ring = sb("e_ring", [P, 2 + PACK, HALF], F32)
-        e_sum = [e_ring[:, 2 : 2 + PACK, :], e_ring[:, 0:PACK, 0:UNIT], e_ring[:, 0:PACK, UNIT:HALF]]
+        e_sum = [e_ring[:, 2 : 2 + PACK, 0:HALF], e_ring[:, 0:PACK, 0:UNIT], e_ring[:, 0:PACK, UNIT:HALF]]
 
         oq = sb("oq", [P, S], U32)
         osc = sb("osc", [P, S], U8)
@@ -237,9 +247,8 @@ def tile_picked_glutap_none_po_kernel(
 
         def gather_e(c, t):
             a, b = CHUNKS[c]
-            nc.vector.tensor_tensor(
-                e_sum[c][:, t, :], e_win[t][:].indirect(entries(tap_sb, a, b)), e_dup[t][:, a:b], ADD
-            )
+            plain = e_low[t] if c == 0 else e_high[t][:, a - HALF : b - HALF]
+            nc.vector.tensor_tensor(e_sum[c][:, t, :], e_win[t][:].indirect(entries(tap_sb, a, b)), plain, ADD)
 
         def gated(c, u):
             off = u * UNIT - CHUNKS[c][0]
@@ -286,8 +295,11 @@ def tile_picked_glutap_none_po_kernel(
                 o_bf[u][:].rearrange("p (c i) t -> p c t i", i=4),
                 acc[:].rearrange("p t (c i) -> p c t i", i=4),
             )
-            nc.scalar.copy(o_f32[u][:], acc[:])
-            nc.scalar.dma_start(out_rows[:, :, u * UNIT : (u + 1) * UNIT], o_f32[u][:])
+            for t0, queue in ((0, nc.sync), (2, nc.scalar)):
+                nc.scalar.copy(o_f32[u][:, t0 : t0 + 2, :], acc[:, t0 : t0 + 2, :])
+                queue.dma_start(
+                    out_rows[:, t0 : t0 + 2, u * UNIT : (u + 1) * UNIT], o_f32[u][:, t0 : t0 + 2, :]
+                )
 
         def hand_on(u):
             a, b = u * UNIT, (u + 1) * UNIT

@@ -199,17 +199,14 @@ def tile_picked_glutap_none_po_kernel(
             nc.gpsimd.tensor_copy(dealt[:], raw[:].rearrange("p (m t) -> p t m", t=PACK))
 
         e_win = [sb(f"e_win{t}", [P, S], F32) for t in range(PACK)]
-        e_ring = late.tile([P, 2 + PACK, HALF], F32, name="e_ring", offset=9 * H, align_bytes=64)
-        e_low = [e_ring[:, PACK, :], e_ring[:, PACK + 1, :]] + [sb(f"e_low{t}", [P, HALF], F32)[:] for t in (2, 3)]
+        e_ring = sb("e_ring", [P, 2 + PACK, HALF], F32)
+        e_low = [sb(f"e_low{t}", [P, HALF], F32)[:] for t in range(PACK)]
         e_high = [sb(f"e_high{t}", [P, HALF], F32)[:] for t in range(PACK)]
         e_acc = {}
 
         def empty_e(t):
             nc.scalar.copy(e_win[t][:], e_acc[t][:])
-            if t < 2:
-                nc.gpsimd.tensor_copy(e_low[t], e_win[t][:, 0:HALF])
-            else:
-                nc.scalar.copy(e_low[t], e_acc[t][:, 0:HALF])
+            nc.scalar.copy(e_low[t], e_acc[t][:, 0:HALF])
             nc.sync.dma_start(e_high[t], e_win[t][:, HALF:S])
 
         for t in (0, 1):

@@ -19,6 +19,7 @@ PACK = 4
 T, S, H = 2048, 512, 512
 HALF = S // 2
 UNIT = 128
+PIECE = UNIT // 2
 FLOPS = 3 * 2 * 512 * 512 * 512
 CHUNKS = ((0, 256), (256, 384), (384, 512))
 
@@ -247,25 +248,27 @@ def tile_picked_glutap_none_po_kernel(
             plain = e_low[t] if c == 0 else e_high[t][:, a - HALF : b - HALF]
             nc.vector.tensor_tensor(e_sum[c][:, t, :], e_win[t][:].indirect(entries(tap_sb, a, b)), plain, ADD)
 
-        def gated(c, u):
+        def gated(c, u, a=0, b=UNIT):
             off = u * UNIT - CHUNKS[c][0]
             nc.vector.tensor_tensor(
-                z_bf[u][:].rearrange("p (c i) t -> p c t i", i=4),
-                e_sum[c][:, :, off : off + UNIT].rearrange("p t (c i) -> p c t i", i=4),
-                gate[u][:].rearrange("p t (c i) -> p c t i", i=4),
+                z_bf[u][:, a:b, :].rearrange("p (c i) t -> p c t i", i=4),
+                e_sum[c][:, :, off + a : off + b].rearrange("p t (c i) -> p c t i", i=4),
+                gate[u][:, :, a:b].rearrange("p t (c i) -> p c t i", i=4),
                 MULT,
             )
             nc.vector.quantize_mx(
-                out=zq[u][:].bitcast(FP8X4), scales=zs[u][:], in_=z_bf[u][:].rearrange("p n t -> p (n t)")
+                out=zq[u][:, a:b].bitcast(FP8X4),
+                scales=zs[u][:, a:b],
+                in_=z_bf[u][:, a:b, :].rearrange("p n t -> p (n t)"),
             )
 
-        def product(dst, t, u):
+        def product(dst, t, u, a=0, b=UNIT):
             nc.tensor.matmul_mx(
                 dst,
                 lhsT=w3q[:, t, :].bitcast(FP8X4),
                 lhsT_scale=w3s[:, t, :],
-                rhs=zq[u][:].bitcast(FP8X4),
-                rhs_scale=zs[u][:],
+                rhs=zq[u][:, a:b].bitcast(FP8X4),
+                rhs_scale=zs[u][:, a:b],
                 start=True,
                 stop=True,
             )
@@ -283,20 +286,17 @@ def tile_picked_glutap_none_po_kernel(
         def empty_bank(u):
             nc.scalar.copy(o_bf[u][:], o_bank[u][:].rearrange("p t n -> p n t"))
 
-        def last_layer_in_two_banks(u):
-            acc = bank(4, [P, PACK, UNIT])
-            for t in range(PACK):
-                product(acc[:, t, :], t, u)
-            o_bf[u] = sb("o_bf1", [P, UNIT, PACK], BF16)
+        def round_walk(dst, src):
             nc.vector.tensor_copy(
-                o_bf[u][:].rearrange("p (c i) t -> p c t i", i=4),
-                acc[:].rearrange("p t (c i) -> p c t i", i=4),
+                dst.rearrange("p (c i) t -> p c t i", i=4), src.rearrange("p t (c i) -> p c t i", i=4)
             )
-            for t0, queue in ((0, nc.sync), (2, nc.scalar)):
-                nc.scalar.copy(o_f32[u][:, t0 : t0 + 2, :], acc[:, t0 : t0 + 2, :])
-                queue.dma_start(
-                    out_rows[:, t0 : t0 + 2, u * UNIT : (u + 1) * UNIT], o_f32[u][:, t0 : t0 + 2, :]
-                )
+
+        def last_piece(u, a, b, k):
+            acc = bank(k, [P, PACK, b - a])
+            for t in range(PACK):
+                product(acc[:, t, :], t, u, a, b)
+            round_walk(o_bf[u][:, a:b, :], acc[:])
+            nc.scalar.copy(o_f32[u][:, :, a:b], acc[:])
 
         def hand_on(u):
             a, b = u * UNIT, (u + 1) * UNIT
@@ -326,17 +326,22 @@ def tile_picked_glutap_none_po_kernel(
             gather_e(1, t)
         gated(1, 2)
         last_layer(2)
-        empty_bank(2)
+        nc.scalar.copy(o_bf[2][:, 0:PIECE, :], o_bank[2][:, :, 0:PIECE].rearrange("p t n -> p n t"))
         for t in range(PACK):
             gather_e(2, t)
-        gated(2, 3)
+        for a in (0, PIECE):
+            gated(2, 3, a, a + PIECE)
         for u in range(2):
             hand_on(u)
-        last_layer_in_two_banks(3)
-        for u in range(2, 4):
+        o_bf[3] = sb("o_bf1", [P, UNIT, PACK], BF16)
+        last_piece(3, 0, PIECE, 4)
+        last_piece(3, PIECE, UNIT, 6)
+        nc.scalar.dma_start(out_rows[:, :, 3 * UNIT : S], o_f32[3][:])
+        round_walk(o_bf[2][:, PIECE:UNIT, :], o_f32[2][:, :, PIECE:UNIT])
+        for u in (3, 2):
             hand_on(u)
         for a, b in ((0, HALF), (HALF, S)):
             nc.sync.dma_start(out_words[:, a:b], oq[:, a:b].bitcast(I32))
         for q in range(4):
-            queue = nc.scalar if q == 3 else nc.sync
+            queue = nc.scalar if q >= 2 else nc.sync
             queue.dma_start(out_2[0, q:16:4, :].bitcast(I32), osc[q:P:32, :].bitcast(I32))

@@ -13,6 +13,7 @@ FP8X4 = mybir.dt.float8_e4m3fn_x4
 ADD = mybir.AluOpType.add
 MULT = mybir.AluOpType.mult
 SIGMOID = mybir.ActivationFunctionType.Sigmoid
+COPY = mybir.ActivationFunctionType.Copy
 
 P = 128
 PACK = 4
@@ -202,7 +203,8 @@ def tile_picked_glutap_none_po_kernel(
         e_win = [sb(f"e_win{t}", [P, S], F32) for t in range(PACK)]
         e_ring = sb("e_ring", [P, 2 + PACK, HALF], F32)
         e_low = [sb(f"e_low{t}", [P, HALF], F32)[:] for t in range(PACK)]
-        e_high = [sb(f"e_high{t}", [P, HALF], F32)[:] for t in range(PACK)]
+        e_high_all = sb("e_high", [P, PACK, HALF], F32)
+        e_high = [e_high_all[:, t, :] for t in range(PACK)]
         e_acc = {}
 
         def empty_e(t):
@@ -247,6 +249,13 @@ def tile_picked_glutap_none_po_kernel(
             a, b = CHUNKS[c]
             plain = e_low[t] if c == 0 else e_high[t][:, a - HALF : b - HALF]
             nc.vector.tensor_tensor(e_sum[c][:, t, :], e_win[t][:].indirect(entries(tap_sb, a, b)), plain, ADD)
+
+        def gather_e_apart(c):
+            a, b = CHUNKS[c]
+            e_tap = sb(f"e_tap{c}", [P, PACK, b - a], F32)
+            for t in range(PACK):
+                nc.scalar.activation(e_tap[:, t, :], e_win[t][:].indirect(entries(tap_sb, a, b)), COPY)
+            nc.vector.tensor_tensor(e_sum[c], e_tap[:], e_high_all[:, :, a - HALF : b - HALF], ADD)
 
         def gated(c, u, a=0, b=UNIT):
             off = u * UNIT - CHUNKS[c][0]
@@ -308,6 +317,8 @@ def tile_picked_glutap_none_po_kernel(
             gather_e(0, t)
         for u in (0, 1):
             gated(0, u)
+        gather_e_apart(2)
+        for u in (0, 1):
             last_layer(u)
         spare = bank(5, [P, S])
         for k in range(3):
@@ -327,8 +338,6 @@ def tile_picked_glutap_none_po_kernel(
         gated(1, 2)
         last_layer(2)
         nc.scalar.copy(o_bf[2][:, 0:PIECE, :], o_bank[2][:, :, 0:PIECE].rearrange("p t n -> p n t"))
-        for t in range(PACK):
-            gather_e(2, t)
         for a in (0, PIECE):
             gated(2, 3, a, a + PIECE)
         for u in range(2):

@@ -241,7 +241,7 @@ def tile_picked_glutap_none_po_kernel(
         z_bf = [sb(f"z_bf{u}", [P, UNIT, PACK], BF16) for u in units]
         zq = [sb(f"zq{u}", [P, UNIT], U32) for u in units]
         zs = [sb(f"zs{u}", [P, UNIT], U8) for u in units]
-        o_bf = {u: sb(f"o_bf{u}", [P, UNIT, PACK], BF16) for u in range(3)}
+        o_bf = {u: sb(f"o_bf{u}", [P, UNIT, PACK], BF16) for u in (0, 2)}
         o_f32 = [sb(f"o_f32{u}", [P, PACK, UNIT], F32) for u in units]
         o_bank = {}
 
@@ -331,8 +331,7 @@ def tile_picked_glutap_none_po_kernel(
                 start=True,
                 stop=True,
             )
-        for u in (0, 1):
-            empty_bank(u)
+        empty_bank(0)
         for t in range(PACK):
             gather_e(1, t)
         gated(1, 2)
@@ -340,9 +339,11 @@ def tile_picked_glutap_none_po_kernel(
         nc.scalar.copy(o_bf[2][:, 0:PIECE, :], o_bank[2][:, :, 0:PIECE].rearrange("p t n -> p n t"))
         for a in (0, PIECE):
             gated(2, 3, a, a + PIECE)
-        for u in range(2):
-            hand_on(u)
-        o_bf[3] = sb("o_bf1", [P, UNIT, PACK], BF16)
+        hand_on(0)
+        o_bf[1] = sb("z_bf2", [P, UNIT, PACK], BF16)
+        round_walk(o_bf[1][:], o_f32[1][:])
+        hand_on(1)
+        o_bf[3] = sb("o_bf0", [P, UNIT, PACK], BF16)
         last_piece(3, 0, PIECE, 4)
         last_piece(3, PIECE, UNIT, 6)
         nc.scalar.dma_start(out_rows[:, :, 3 * UNIT : S], o_f32[3][:])

@@ -201,7 +201,7 @@ def tile_picked_glutap_none_po_kernel(
             nc.gpsimd.tensor_copy(dealt[:], raw[:].rearrange("p (m t) -> p t m", t=PACK))
 
         e_win = [sb(f"e_win{t}", [P, S], F32) for t in range(PACK)]
-        e_ring = sb("e_ring", [P, 2 + PACK, HALF], F32)
+        e_ring = turns.tile([P, 2 + PACK, HALF], F32, name="e_ring", offset=24 * S, align_bytes=64)
         e_low = [sb(f"e_low{t}", [P, HALF], F32)[:] for t in range(PACK)]
         e_high_all = sb("e_high", [P, PACK, HALF], F32)
         e_high = [e_high_all[:, t, :] for t in range(PACK)]
@@ -231,7 +231,7 @@ def tile_picked_glutap_none_po_kernel(
             for t in range(PACK):
                 gate_back(t, u)
 
-        e_sum = [e_ring[:, 2 : 2 + PACK, 0:HALF], e_ring[:, 0:PACK, 0:UNIT], e_ring[:, 0:PACK, UNIT:HALF]]
+        e_sum = [e_ring[:, 2 : 2 + PACK, 0:HALF], e_ring[:, 0:PACK, UNIT:HALF], e_ring[:, 0:PACK, 0:UNIT]]
 
         oq = sb("oq", [P, S], U32)
         osc = sb("osc", [P, S], U8)
@@ -307,6 +307,17 @@ def tile_picked_glutap_none_po_kernel(
             round_walk(o_bf[u][:, a:b, :], acc[:])
             nc.scalar.copy(o_f32[u][:, :, a:b], acc[:])
 
+        def warm_up(u):
+            nc.tensor.matmul_mx(
+                spare[:],
+                lhsT=zq[u][:].bitcast(FP8X4),
+                lhsT_scale=zs[u][:],
+                rhs=w3q[:].rearrange("p t m -> p (t m)").bitcast(FP8X4),
+                rhs_scale=w3s[:].rearrange("p t m -> p (t m)"),
+                start=True,
+                stop=True,
+            )
+
         def hand_on(u):
             a, b = u * UNIT, (u + 1) * UNIT
             nc.vector.quantize_mx(
@@ -317,38 +328,31 @@ def tile_picked_glutap_none_po_kernel(
             gather_e(0, t)
         for u in (0, 1):
             gated(0, u)
-        gather_e_apart(2)
+        gather_e_apart(1)
         for u in (0, 1):
             last_layer(u)
         spare = bank(5, [P, S])
-        for k in range(3):
-            nc.tensor.matmul_mx(
-                spare[:],
-                lhsT=zq[1][:].bitcast(FP8X4),
-                lhsT_scale=zs[1][:],
-                rhs=w3q[:].rearrange("p t m -> p (t m)").bitcast(FP8X4),
-                rhs_scale=w3s[:].rearrange("p t m -> p (t m)"),
-                start=True,
-                stop=True,
-            )
+        for k in range(2):
+            warm_up(1)
         empty_bank(0)
-        for t in range(PACK):
-            gather_e(1, t)
+        for t in range(3):
+            gather_e(2, t)
         gated(1, 2)
+        gather_e(2, 3)
         last_layer(2)
-        nc.scalar.copy(o_bf[2][:, 0:PIECE, :], o_bank[2][:, :, 0:PIECE].rearrange("p t n -> p n t"))
+        warm_up(2)
+        empty_bank(2)
         for a in (0, PIECE):
             gated(2, 3, a, a + PIECE)
         hand_on(0)
-        o_bf[1] = sb("z_bf2", [P, UNIT, PACK], BF16)
+        o_bf[1] = turns.tile([P, UNIT, PACK], BF16, name="o_bf1", offset=24 * S, align_bytes=64)
         round_walk(o_bf[1][:], o_f32[1][:])
         hand_on(1)
         o_bf[3] = sb("o_bf0", [P, UNIT, PACK], BF16)
         last_piece(3, 0, PIECE, 4)
         last_piece(3, PIECE, UNIT, 6)
         nc.scalar.dma_start(out_rows[:, :, 3 * UNIT : S], o_f32[3][:])
-        round_walk(o_bf[2][:, PIECE:UNIT, :], o_f32[2][:, :, PIECE:UNIT])
-        for u in (3, 2):
+        for u in (2, 3):
             hand_on(u)
         for a, b in ((0, HALF), (HALF, S)):
             nc.sync.dma_start(out_words[:, a:b], oq[:, a:b].bitcast(I32))

@@ -23,6 +23,8 @@ UNIT = 128
 PIECE = UNIT // 2
 FLOPS = 3 * 2 * 512 * 512 * 512
 CHUNKS = ((0, 256), (256, 384), (384, 512))
+OUT_BANKS = (2, 5, 6)
+RAW_AT, W1Q_AT, W2Q_AT, RING_AT = 0, 4096, 6144, 8192
 
 
 def tile_picked_glutap_none_po_kernel(
@@ -58,12 +60,12 @@ def tile_picked_glutap_none_po_kernel(
         w1s = sb("w1s", [P, PACK, P], U8)
         xs = sb("xs", [P, S], U8)
         w1_raw = sb("w1_raw", [P, H], U32)
-        w3_raw = late.tile([P, H], U32, name="w3_raw", offset=9 * H, align_bytes=64)
+        w3_raw = sb("w3_raw", [P, H], U32)
         w1s_raw = sb("w1s_raw", [P, H], U8)
-        w3s_raw = late.tile([P, H], U8, name="w3s_raw", offset=8 * H, align_bytes=64)
+        w3s_raw = sb("w3s_raw", [P, H], U8)
         w2_raw = [
-            sb("w2_raw0", [P, PACK, H // 2], F32)[:],
-            turns.tile([P, 6 * S], F32, name="w2_raw1", offset=0)[:, 0 : 2 * S].rearrange("p (j c) -> p j c", j=PACK),
+            sb("w2_raw0", [P, PACK, H // 2], F32),
+            turns.tile([P, PACK, H // 2], F32, name="w2_raw1", offset=RAW_AT, align_bytes=64),
         ]
         warm_out = sb("warm_out", [P, 16], F32)
         ident = sb("ident", [P, P], F32)
@@ -82,25 +84,16 @@ def tile_picked_glutap_none_po_kernel(
         nc.sync.dma_start(x_tab[:].bitcast(I32), words_view(x_words))
         nc.scalar.activation(warm_out[:], ident[:, 0:16], SIGMOID)
 
-        def deal(name, raw, dtype):
-            dealt = sb(name, [P, PACK, P], dtype)
-            if dtype == U8:
-                nc.vector.tensor_copy(dealt[:], raw[:].rearrange("p (m t) -> p t m", t=PACK))
-            else:
-                nc.vector.tensor_copy(
-                    dealt[:].rearrange("p t m -> p m t"), raw[:].rearrange("p (m t) -> p m t", t=PACK)
-                )
-            return dealt
-
-        w1q = deal("w1q", w1_raw, U32)
+        w1q = turns.tile([P, PACK, P], U32, name="w1q", offset=W1Q_AT, align_bytes=64)
+        nc.vector.tensor_copy(w1q[:].rearrange("p t m -> p m t"), w1_raw[:].rearrange("p (m t) -> p m t", t=PACK))
         nc.vector.tensor_copy(xs[:], xs_tab[:].indirect(offs_sb[:]))
         load_scale_rows(nc.sync, w1s_raw, w1_scales)
         w1s_slices = w1s_raw[:].rearrange("p (m t) -> p t m", t=PACK)
         for t0, t1 in ((0, 1), (1, PACK)):
             nc.gpsimd.tensor_copy(w1s[:, t0:t1, :], w1s_slices[:, t0:t1, :])
-        nc.sync.dma_start(w2_raw[0], w2_rows[:, :, 0 : H // 2])
+        nc.sync.dma_start(w2_raw[0][:], w2_rows[:, :, 0 : H // 2])
         nc.sync.dma_start(tap_sb[:], tap)
-        nc.sync.dma_start(w2_raw[1], w2_rows[:, :, H // 2 : H])
+        nc.sync.dma_start(w2_raw[1][:], w2_rows[:, :, H // 2 : H])
         nc.sync.dma_start(w3_raw[:].bitcast(I32), words_view(w3_words))
         load_scale_rows(nc.sync, w3s_raw, w3_scales)
 
@@ -124,112 +117,117 @@ def tile_picked_glutap_none_po_kernel(
 
         w2_bf = late.tile([P, PACK, P, PACK], BF16, name="w2_bf", offset=0, align_bytes=64)
 
-        def round_w2(h, g0, g1, copy):
+        def w2_views(h):
             m0 = h * P // 2
-            copy(
-                w2_bf[:, :, m0 + g0 : m0 + g1, :].rearrange("p t m j -> p m t j"),
-                w2_raw[h][:, :, PACK * g0 : PACK * g1].rearrange("p j (m t) -> p m t j", t=PACK),
+            return (
+                w2_bf[:, :, m0 : m0 + P // 2, :].rearrange("p t m j -> p m t j"),
+                w2_raw[h][:].rearrange("p j (m t) -> p m t j", t=PACK),
             )
 
-        y_win = {}
-        for t in range(2):
-            y_win[t] = sb(f"y_win{t}", [P, 2 * S], F32)
-        for (a, b), k in zip(CHUNKS, (0, 1, 7)):
+        y_win = [sb(f"y_win{t}", [P, S], F32) for t in range(PACK)]
+        for k, (a, b) in enumerate(CHUNKS):
             acc = project(w1q, w1s, 0, a, b, k)
             nc.scalar.copy(y_win[0][:, a:b], acc[:, 0 : b - a])
-        y_acc = {t: project(w1q, w1s, t, 0, S, 1 + t) for t in range(1, PACK)}
-        nc.scalar.copy(y_win[1][:, 0:S], y_acc[1][:])
-        round_w2(0, 0, 64, nc.vector.tensor_copy)
-        round_w2(1, 0, 32, nc.scalar.copy)
-        round_w2(1, 32, 64, nc.gpsimd.tensor_copy)
-        for t in (2, 3):
-            y_win[t] = turns.tile([P, 2 * S], F32, name=f"y_win{t}", offset=8 * S * (t - 2))
-            nc.scalar.copy(y_win[t][:, 0:S], y_acc[t][:])
+        for t in range(1, PACK):
+            acc = project(w1q, w1s, t, 0, S, 2 + t)
+            nc.scalar.copy(y_win[t][:], acc[:])
+        nc.vector.tensor_copy(*w2_views(0))
+        nc.gpsimd.tensor_scalar(*w2_views(1), 1.0, 0.0, MULT, ADD)
 
         y_tap = {}
         sum_bank = {}
+        gate_turned = {}
         gate = {}
 
-        def gather_y(t, name):
-            y_tap[t] = sb(name, [P, S], F32)
-            nc.vector.tensor_copy(y_tap[t][:], y_win[t][:].indirect(tap_sb[:]))
+        def cols(u):
+            return slice(u * UNIT, (u + 1) * UNIT)
 
-        def add_turned(t, k):
-            sum_bank[t] = bank(k, [P, S])
-            for u in range(PACK):
-                cols = slice(u * UNIT, (u + 1) * UNIT)
-                nc.tensor.matmul(
-                    sum_bank[t][:, cols], y_win[t][:, cols], ident[:], start=(u == 0), stop=False, is_transpose=True
-                )
-            for u in range(PACK):
-                cols = slice(u * UNIT, (u + 1) * UNIT)
-                nc.tensor.matmul(
-                    sum_bank[t][:, cols], y_tap[t][:, cols], ident[:], start=False, stop=(u == PACK - 1), is_transpose=True
-                )
-
-        gate_turned = {}
-
-        def squash(t):
-            if t < 2:
-                gate_turned[t] = turns.tile([P, S], F32, name=f"gate_turned{t}", offset=16 * S + 4 * S * t)[:]
+        def add_turned(u, k, taps_first):
+            sum_bank[u] = bank(k, [P, PACK, P])
+            plain = [(t, y_win[t][:, cols(u)]) for t in range(PACK)]
+            taps = [(t, y_tap[t, u]) for t in range(PACK)]
+            if taps_first:
+                steps = taps[1:] + taps[:1] + plain
             else:
-                gate_turned[t] = y_win[t][:, S : 2 * S]
+                steps = [step for pair in zip(plain, taps) for step in pair]
+            for i, (t, src) in enumerate(steps):
+                nc.tensor.matmul(
+                    sum_bank[u][:, t, :], src, ident[:], start=(i == 0), stop=(i == len(steps) - 1), is_transpose=True
+                )
 
-        def squash_columns(t, a, b):
-            nc.scalar.activation(gate_turned[t][:, a:b], sum_bank[t][:, a:b], SIGMOID)
+        def squash(u, dst):
+            gate_turned[u] = dst
+            nc.scalar.activation(dst[:], sum_bank[u][:], SIGMOID)
 
-        def gate_back(t, u):
-            if t == 0:
-                gate[u] = bank((5 + u) % 8, [P, PACK, UNIT])
-            nc.tensor.transpose(gate[u][:, t, :], gate_turned[t][:, u * UNIT : (u + 1) * UNIT], ident[:])
+        def gate_back(u, k):
+            gate[u] = bank(k, [P, PACK, UNIT])
+            for t in range(PACK):
+                nc.tensor.transpose(gate[u][:, t, :], gate_turned[u][:, t, :], ident[:])
 
-        gather_y(0, "y_tap0")
-        gather_y(1, "y_tap1")
+        def gather_low(t, low):
+            nc.vector.tensor_copy(low[:], y_win[t][:].indirect(entries(tap_sb, 0, HALF)))
+            y_tap[t, 0], y_tap[t, 1] = low[:, cols(0)], low[:, cols(1)]
 
-        w2q = sb("w2q", [P, PACK, P], U32)
+        def gather_third(t, third):
+            nc.vector.tensor_copy(third[:], y_win[t][:].indirect(entries(tap_sb, HALF, 3 * UNIT)))
+            y_tap[t, 2] = third[:]
+
+        gather_low(0, sb("y_low0", [P, HALF], F32))
+        gather_third(0, sb("y_third0", [P, UNIT], F32))
+        gather_low(1, sb("y_low1", [P, HALF], F32))
+        for t in range(PACK):
+            last = turns.tile([P, UNIT], F32, name=f"y_last{t}", offset=W1Q_AT + 4 * UNIT * t, align_bytes=64)
+            nc.scalar.activation(last[:], y_win[t][:].indirect(entries(tap_sb, 3 * UNIT, S)), COPY)
+            y_tap[t, 3] = last[:]
+
+        w2q = turns.tile([P, PACK, P], U32, name="w2q", offset=W2Q_AT, align_bytes=64)
         w2s = sb("w2s", [P, PACK, P], U8)
         nc.vector.quantize_mx(
             out=w2q[:].rearrange("p t m -> p (t m)").bitcast(FP8X4),
             scales=w2s[:].rearrange("p t m -> p (t m)"),
             in_=w2_bf[:].rearrange("p t m j -> p (t m j)"),
         )
-        gather_y(2, "y_tap2")
-        gather_y(3, "y_tap3")
-        w3q = late.tile([P, PACK, P], U32, name="w3q", offset=4 * H + 64, align_bytes=64)
-        w3s = sb("w3s", [P, PACK, P], U8)
+        e_acc = [project(w2q, w2s, t, 0, S, t) for t in range(PACK)]
+        for t in (2, 3):
+            gather_low(t, turns.tile([P, HALF], F32, name=f"y_low{t}", offset=RAW_AT + 4 * HALF * t, align_bytes=64))
+        for t in range(1, PACK):
+            gather_third(t, turns.tile([P, UNIT], F32, name=f"y_third{t}", offset=RAW_AT + 4 * UNIT * t, align_bytes=64))
+        w3q = late.tile([P, PACK, P], U32, name="w3q", offset=0, align_bytes=64)
+        w3s = late.tile([P, PACK, P], U8, name="w3s", offset=4 * H, align_bytes=64)
         for dealt, raw in ((w3s, w3s_raw), (w3q, w3_raw)):
             nc.gpsimd.tensor_copy(dealt[:], raw[:].rearrange("p (m t) -> p t m", t=PACK))
 
         e_win = [sb(f"e_win{t}", [P, S], F32) for t in range(PACK)]
-        e_ring = turns.tile([P, 2 + PACK, HALF], F32, name="e_ring", offset=24 * S, align_bytes=64)
+        e_ring = turns.tile([P, 2 + PACK, HALF], F32, name="e_ring", offset=RING_AT, align_bytes=64)
         e_low = [sb(f"e_low{t}", [P, HALF], F32)[:] for t in range(PACK)]
         e_high_all = sb("e_high", [P, PACK, HALF], F32)
         e_high = [e_high_all[:, t, :] for t in range(PACK)]
-        e_acc = {}
 
-        def empty_e(t):
-            nc.scalar.copy(e_win[t][:], e_acc[t][:])
-            nc.scalar.copy(e_low[t], e_acc[t][:, 0:HALF])
+        def window_e(t, copy):
+            copy(e_win[t][:], e_acc[t][:])
             nc.sync.dma_start(e_high[t], e_win[t][:, HALF:S])
 
-        for t in (0, 1):
-            add_turned(t, 5 + t)
-        for t in (0, 1):
-            squash(t)
-            squash_columns(t, 0, S)
-        for t in range(PACK):
-            e_acc[t] = project(w2q, w2s, t, 0, S, 1 + t)
-        for t in range(PACK):
-            empty_e(t)
+        def twin_e(t):
+            nc.scalar.copy(e_low[t], e_acc[t][:, 0:HALF])
+
+        add_turned(0, 6, False)
+        window_e(0, nc.scalar.copy)
+        twin_e(1)
+        twin_e(0)
+        window_e(1, nc.vector.tensor_copy)
+        squash(0, sb("gate_turned0", [P, PACK, P], F32))
         for t in (2, 3):
-            add_turned(t, (5 + t) % 8)
-            squash(t)
-        for a, b in ((0, HALF), (HALF, S)):
-            for t in (2, 3):
-                squash_columns(t, a, b)
-        for u in range(PACK):
-            for t in range(PACK):
-                gate_back(t, u)
+            window_e(t, nc.scalar.copy)
+            twin_e(t)
+
+        add_turned(1, 0, False)
+        gate_back(0, 1)
+        add_turned(2, 4, True)
+        squash(1, turns.tile([P, PACK, P], F32, name="gate_turned1", offset=W2Q_AT, align_bytes=64))
+        squash(2, sb("gate_turned2", [P, PACK, P], F32))
+        add_turned(3, 3, False)
+        gate_back(1, 0)
+        gate_back(2, 4)
 
         e_sum = [e_ring[:, 2 : 2 + PACK, 0:HALF], e_ring[:, 0:PACK, UNIT:HALF], e_ring[:, 0:PACK, 0:UNIT]]
 
@@ -286,7 +284,7 @@ def tile_picked_glutap_none_po_kernel(
             nc.sync.dma_start(out_rows[:, :, u * UNIT : (u + 1) * UNIT], o_f32[u][:])
 
         def last_layer(u):
-            o_bank[u] = bank(1 + u, [P, PACK, UNIT])
+            o_bank[u] = bank(OUT_BANKS[u], [P, PACK, UNIT])
             for t in range(PACK):
                 product(o_bank[u][:, t, :], t, u)
             nc.scalar.copy(o_f32[u][:], o_bank[u][:])
@@ -307,17 +305,6 @@ def tile_picked_glutap_none_po_kernel(
             round_walk(o_bf[u][:, a:b, :], acc[:])
             nc.scalar.copy(o_f32[u][:, :, a:b], acc[:])
 
-        def warm_up(u):
-            nc.tensor.matmul_mx(
-                spare[:],
-                lhsT=zq[u][:].bitcast(FP8X4),
-                lhsT_scale=zs[u][:],
-                rhs=w3q[:].rearrange("p t m -> p (t m)").bitcast(FP8X4),
-                rhs_scale=w3s[:].rearrange("p t m -> p (t m)"),
-                start=True,
-                stop=True,
-            )
-
         def hand_on(u):
             a, b = u * UNIT, (u + 1) * UNIT
             nc.vector.quantize_mx(
@@ -329,28 +316,26 @@ def tile_picked_glutap_none_po_kernel(
         for u in (0, 1):
             gated(0, u)
         gather_e_apart(1)
+        squash(3, sb("gate_turned3", [P, PACK, P], F32))
+        gate_back(3, 3)
         for u in (0, 1):
             last_layer(u)
-        spare = bank(5, [P, S])
-        for k in range(2):
-            warm_up(1)
         empty_bank(0)
         for t in range(3):
             gather_e(2, t)
         gated(1, 2)
         gather_e(2, 3)
         last_layer(2)
-        warm_up(2)
         empty_bank(2)
         for a in (0, PIECE):
             gated(2, 3, a, a + PIECE)
         hand_on(0)
-        o_bf[1] = turns.tile([P, UNIT, PACK], BF16, name="o_bf1", offset=24 * S, align_bytes=64)
+        o_bf[1] = turns.tile([P, UNIT, PACK], BF16, name="o_bf1", offset=RING_AT, align_bytes=64)
         round_walk(o_bf[1][:], o_f32[1][:])
         hand_on(1)
         o_bf[3] = sb("o_bf0", [P, UNIT, PACK], BF16)
-        last_piece(3, 0, PIECE, 4)
-        last_piece(3, PIECE, UNIT, 6)
+        last_piece(3, 0, PIECE, 7)
+        last_piece(3, PIECE, UNIT, 1)
         nc.scalar.dma_start(out_rows[:, :, 3 * UNIT : S], o_f32[3][:])
         for u in (2, 3):
             hand_on(u)

@@ -24,7 +24,7 @@ PIECE = UNIT // 2
 FLOPS = 3 * 2 * 512 * 512 * 512
 CHUNKS = ((0, 256), (256, 384), (384, 512))
 OUT_BANKS = (2, 5, 6)
-RAW_AT, W1Q_AT, W2Q_AT, RING_AT = 0, 4096, 6144, 8192
+RAW_AT, W1Q_AT, W2Q_AT, Z_AT, RING_AT = 0, 4096, 6144, 9216, 13312
 
 
 def tile_picked_glutap_none_po_kernel(
@@ -98,8 +98,7 @@ def tile_picked_glutap_none_po_kernel(
         load_scale_rows(nc.sync, w3s_raw, w3_scales)
 
         xq = sb("xq", [P, S], U32)
-        for h in range(2):
-            a, b = h * HALF, (h + 1) * HALF
+        for a, b in CHUNKS:
             nc.vector.tensor_copy(xq[:, a:b], x_tab[:].indirect(entries(offs_sb, a, b)))
 
         def project(wq, ws, t, a, b, k):
@@ -198,7 +197,7 @@ def tile_picked_glutap_none_po_kernel(
             nc.gpsimd.tensor_copy(dealt[:], raw[:].rearrange("p (m t) -> p t m", t=PACK))
 
         e_win = [sb(f"e_win{t}", [P, S], F32) for t in range(PACK)]
-        e_ring = turns.tile([P, 2 + PACK, HALF], F32, name="e_ring", offset=RING_AT, align_bytes=64)
+        e_rows = turns.tile([P, 29, UNIT], F32, name="e_rows", offset=RING_AT, align_bytes=64)
         e_low = [sb(f"e_low{t}", [P, HALF], F32)[:] for t in range(PACK)]
         e_high_all = sb("e_high", [P, PACK, HALF], F32)
         e_high = [e_high_all[:, t, :] for t in range(PACK)]
@@ -229,14 +228,14 @@ def tile_picked_glutap_none_po_kernel(
         gate_back(1, 0)
         gate_back(2, 4)
 
-        e_sum = [e_ring[:, 2 : 2 + PACK, 0:HALF], e_ring[:, 0:PACK, UNIT:HALF], e_ring[:, 0:PACK, 0:UNIT]]
+        e_sum = [e_rows[:, 1:9, :].rearrange("p (t h) n -> p t (h n)", h=2), e_rows[:, 25:29, :], e_rows[:, 0:25:8, :]]
 
         oq = sb("oq", [P, S], U32)
         osc = sb("osc", [P, S], U8)
         out_rows = out_0.rearrange("(p t) n -> p t n", t=PACK)
         out_words = words_view(out_1)
         units = range(S // UNIT)
-        z_bf = [sb(f"z_bf{u}", [P, UNIT, PACK], BF16) for u in units]
+        z_bf = [turns.tile([P, UNIT, PACK], BF16, name=f"z_bf{u}", offset=Z_AT + 8 * UNIT * u, align_bytes=64) for u in units]
         zq = [sb(f"zq{u}", [P, UNIT], U32) for u in units]
         zs = [sb(f"zs{u}", [P, UNIT], U8) for u in units]
         o_bf = {u: sb(f"o_bf{u}", [P, UNIT, PACK], BF16) for u in (0, 2)}
@@ -250,10 +249,10 @@ def tile_picked_glutap_none_po_kernel(
 
         def gather_e_apart(c):
             a, b = CHUNKS[c]
-            e_tap = sb(f"e_tap{c}", [P, PACK, b - a], F32)
+            e_tap = e_rows[:, 12:25:4, :]
             for t in range(PACK):
                 nc.scalar.activation(e_tap[:, t, :], e_win[t][:].indirect(entries(tap_sb, a, b)), COPY)
-            nc.vector.tensor_tensor(e_sum[c], e_tap[:], e_high_all[:, :, a - HALF : b - HALF], ADD)
+            nc.vector.tensor_tensor(e_sum[c], e_tap, e_high_all[:, :, a - HALF : b - HALF], ADD)
 
         def gated(c, u, a=0, b=UNIT):
             off = u * UNIT - CHUNKS[c][0]
@@ -263,6 +262,8 @@ def tile_picked_glutap_none_po_kernel(
                 gate[u][:, :, a:b].rearrange("p t (c i) -> p c t i", i=4),
                 MULT,
             )
+
+        def quantise_z(u, a=0, b=UNIT):
             nc.vector.quantize_mx(
                 out=zq[u][:, a:b].bitcast(FP8X4),
                 scales=zs[u][:, a:b],
@@ -305,30 +306,32 @@ def tile_picked_glutap_none_po_kernel(
             round_walk(o_bf[u][:, a:b, :], acc[:])
             nc.scalar.copy(o_f32[u][:, :, a:b], acc[:])
 
-        def hand_on(u):
-            a, b = u * UNIT, (u + 1) * UNIT
+        def hand_on(u, a=0, b=UNIT):
+            to = slice(u * UNIT + a, u * UNIT + b)
             nc.vector.quantize_mx(
-                out=oq[:, a:b].bitcast(FP8X4), scales=osc[:, a:b], in_=o_bf[u][:].rearrange("p n t -> p (n t)")
+                out=oq[:, to].bitcast(FP8X4), scales=osc[:, to], in_=o_bf[u][:, a:b, :].rearrange("p n t -> p (n t)")
             )
 
         for t in range(PACK):
             gather_e(0, t)
         for u in (0, 1):
             gated(0, u)
+            quantise_z(u)
         gather_e_apart(1)
-        squash(3, sb("gate_turned3", [P, PACK, P], F32))
-        gate_back(3, 3)
+        squash(3, turns.tile([P, PACK, P], F32, name="gate_turned3", offset=Z_AT - 8 * UNIT, align_bytes=64))
         for u in (0, 1):
             last_layer(u)
+        gate_back(3, 3)
         empty_bank(0)
-        for t in range(3):
-            gather_e(2, t)
         gated(1, 2)
-        gather_e(2, 3)
+        for t in range(PACK):
+            gather_e(2, t)
+        quantise_z(2)
         last_layer(2)
         empty_bank(2)
         for a in (0, PIECE):
             gated(2, 3, a, a + PIECE)
+            quantise_z(3, a, a + PIECE)
         hand_on(0)
         o_bf[1] = turns.tile([P, UNIT, PACK], BF16, name="o_bf1", offset=RING_AT, align_bytes=64)
         round_walk(o_bf[1][:], o_f32[1][:])
@@ -337,8 +340,9 @@ def tile_picked_glutap_none_po_kernel(
         last_piece(3, 0, PIECE, 7)
         last_piece(3, PIECE, UNIT, 1)
         nc.scalar.dma_start(out_rows[:, :, 3 * UNIT : S], o_f32[3][:])
-        for u in (2, 3):
-            hand_on(u)
+        hand_on(2)
+        for a in (0, PIECE):
+            hand_on(3, a, a + PIECE)
         for a, b in ((0, HALF), (HALF, S)):
             nc.sync.dma_start(out_words[:, a:b], oq[:, a:b].bitcast(I32))
         for q in range(4):

@@ -23,7 +23,8 @@ UNIT = 128
 PIECE = UNIT // 2
 FLOPS = 3 * 2 * 512 * 512 * 512
 CHUNKS = ((0, 256), (256, 384), (384, 512))
-OUT_BANKS = (2, 5, 6)
+SUM_BANKS = (6, 7, 0, 1)
+OUT_BANKS = (2, 3, 4)
 RAW_AT, W1Q_AT, W2Q_AT, Z_AT, RING_AT = 0, 4096, 6144, 9216, 13312
 
 
@@ -141,25 +142,35 @@ def tile_picked_glutap_none_po_kernel(
         def cols(u):
             return slice(u * UNIT, (u + 1) * UNIT)
 
-        def add_turned(u, k, taps_first):
-            sum_bank[u] = bank(k, [P, PACK, P])
-            plain = [(t, y_win[t][:, cols(u)]) for t in range(PACK)]
-            taps = [(t, y_tap[t, u]) for t in range(PACK)]
-            if taps_first:
-                steps = taps[1:] + taps[:1] + plain
-            else:
-                steps = [step for pair in zip(plain, taps) for step in pair]
-            for i, (t, src) in enumerate(steps):
-                nc.tensor.matmul(
-                    sum_bank[u][:, t, :], src, ident[:], start=(i == 0), stop=(i == len(steps) - 1), is_transpose=True
-                )
+        turned = {u: 0 for u in range(PACK)}
+
+        def add_turned(u, t, src):
+            if turned[u] == 0:
+                sum_bank[u] = bank(SUM_BANKS[u], [P, PACK, P])
+            nc.tensor.matmul(
+                sum_bank[u][:, t, :],
+                src,
+                ident[:],
+                start=(turned[u] == 0),
+                stop=(turned[u] == 2 * PACK - 1),
+                is_transpose=True,
+            )
+            turned[u] = turned[u] + 1
+
+        def turn_plain(t):
+            for u in range(PACK):
+                add_turned(u, t, y_win[t][:, cols(u)])
+
+        def turn_taps(t, *some_units):
+            for u in some_units:
+                add_turned(u, t, y_tap[t, u])
 
         def squash(u, dst):
             gate_turned[u] = dst
             nc.scalar.activation(dst[:], sum_bank[u][:], SIGMOID)
 
-        def gate_back(u, k):
-            gate[u] = bank(k, [P, PACK, UNIT])
+        def gate_back(u):
+            gate[u] = bank(SUM_BANKS[u], [P, PACK, UNIT])
             for t in range(PACK):
                 nc.tensor.transpose(gate[u][:, t, :], gate_turned[u][:, t, :], ident[:])
 
@@ -168,16 +179,23 @@ def tile_picked_glutap_none_po_kernel(
             y_tap[t, 0], y_tap[t, 1] = low[:, cols(0)], low[:, cols(1)]
 
         def gather_third(t, third):
-            nc.vector.tensor_copy(third[:], y_win[t][:].indirect(entries(tap_sb, HALF, 3 * UNIT)))
-            y_tap[t, 2] = third[:]
+            u = 2 if t < 3 else 3
+            nc.vector.tensor_copy(third[:], y_win[t][:].indirect(entries(tap_sb, u * UNIT, (u + 1) * UNIT)))
+            y_tap[t, u] = third[:]
 
         gather_low(0, sb("y_low0", [P, HALF], F32))
         gather_third(0, sb("y_third0", [P, UNIT], F32))
         gather_low(1, sb("y_low1", [P, HALF], F32))
         for t in range(PACK):
             last = turns.tile([P, UNIT], F32, name=f"y_last{t}", offset=W1Q_AT + 4 * UNIT * t, align_bytes=64)
-            nc.scalar.activation(last[:], y_win[t][:].indirect(entries(tap_sb, 3 * UNIT, S)), COPY)
-            y_tap[t, 3] = last[:]
+            u = 3 if t < 3 else 2
+            nc.scalar.activation(last[:], y_win[t][:].indirect(entries(tap_sb, u * UNIT, (u + 1) * UNIT)), COPY)
+            y_tap[t, u] = last[:]
+        turn_plain(0)
+        turn_taps(0, 0, 1, 2)
+        turn_plain(1)
+        turn_taps(1, 0, 1)
+        turn_plain(2)
 
         w2q = turns.tile([P, PACK, P], U32, name="w2q", offset=W2Q_AT, align_bytes=64)
         w2s = sb("w2s", [P, PACK, P], U8)
@@ -186,7 +204,7 @@ def tile_picked_glutap_none_po_kernel(
             scales=w2s[:].rearrange("p t m -> p (t m)"),
             in_=w2_bf[:].rearrange("p t m j -> p (t m j)"),
         )
-        e_acc = [project(w2q, w2s, t, 0, S, t) for t in range(PACK)]
+        e_acc = [project(w2q, w2s, t, 0, S, 2 + t) for t in range(PACK)]
         for t in (2, 3):
             gather_low(t, turns.tile([P, HALF], F32, name=f"y_low{t}", offset=RAW_AT + 4 * HALF * t, align_bytes=64))
         for t in range(1, PACK):
@@ -209,24 +227,25 @@ def tile_picked_glutap_none_po_kernel(
         def twin_e(t):
             nc.scalar.copy(e_low[t], e_acc[t][:, 0:HALF])
 
-        add_turned(0, 6, False)
+        for u, order in enumerate(((2, 3), (2, 3), (1, 2, 3), (3, 0, 1, 2))):
+            turn_taps(order[0], u)
+            add_turned(u, 3, y_win[3][:, cols(u)])
+            for t in order[1:]:
+                turn_taps(t, u)
         window_e(0, nc.scalar.copy)
         twin_e(1)
         twin_e(0)
         window_e(1, nc.vector.tensor_copy)
+        window_e(2, nc.scalar.copy)
+        twin_e(2)
         squash(0, sb("gate_turned0", [P, PACK, P], F32))
-        for t in (2, 3):
-            window_e(t, nc.scalar.copy)
-            twin_e(t)
-
-        add_turned(1, 0, False)
-        gate_back(0, 1)
-        add_turned(2, 4, True)
+        window_e(3, nc.scalar.copy)
+        twin_e(3)
+        gate_back(0)
         squash(1, turns.tile([P, PACK, P], F32, name="gate_turned1", offset=W2Q_AT, align_bytes=64))
         squash(2, sb("gate_turned2", [P, PACK, P], F32))
-        add_turned(3, 3, False)
-        gate_back(1, 0)
-        gate_back(2, 4)
+        gate_back(1)
+        gate_back(2)
 
         e_sum = [e_rows[:, 1:9, :].rearrange("p (t h) n -> p t (h n)", h=2), e_rows[:, 25:29, :], e_rows[:, 0:25:8, :]]
 
@@ -321,7 +340,7 @@ def tile_picked_glutap_none_po_kernel(
         squash(3, turns.tile([P, PACK, P], F32, name="gate_turned3", offset=Z_AT - 8 * UNIT, align_bytes=64))
         for u in (0, 1):
             last_layer(u)
-        gate_back(3, 3)
+        gate_back(3)
         empty_bank(0)
         gated(1, 2)
         for t in range(PACK):
@@ -337,8 +356,8 @@ def tile_picked_glutap_none_po_kernel(
         round_walk(o_bf[1][:], o_f32[1][:])
         hand_on(1)
         o_bf[3] = sb("o_bf0", [P, UNIT, PACK], BF16)
-        last_piece(3, 0, PIECE, 7)
-        last_piece(3, PIECE, UNIT, 1)
+        last_piece(3, 0, PIECE, 5)
+        last_piece(3, PIECE, UNIT, 6)
         nc.scalar.dma_start(out_rows[:, :, 3 * UNIT : S], o_f32[3][:])
         hand_on(2)
         for a in (0, PIECE):

@@ -325,6 +325,18 @@ def tile_picked_glutap_none_po_kernel(
             round_walk(o_bf[u][:, a:b, :], acc[:])
             nc.scalar.copy(o_f32[u][:, :, a:b], acc[:])
 
+        def warm_up(u, k):
+            spare = bank(k, [P, S])
+            nc.tensor.matmul_mx(
+                spare[:],
+                lhsT=zq[u][:].bitcast(FP8X4),
+                lhsT_scale=zs[u][:],
+                rhs=w3q[:].rearrange("p t m -> p (t m)").bitcast(FP8X4),
+                rhs_scale=w3s[:].rearrange("p t m -> p (t m)"),
+                start=True,
+                stop=True,
+            )
+
         def hand_on(u, a=0, b=UNIT):
             to = slice(u * UNIT + a, u * UNIT + b)
             nc.vector.quantize_mx(
@@ -341,6 +353,7 @@ def tile_picked_glutap_none_po_kernel(
         for u in (0, 1):
             last_layer(u)
         gate_back(3)
+        warm_up(1, 7)
         empty_bank(0)
         gated(1, 2)
         for t in range(PACK):

@@ -24,7 +24,8 @@ PIECE = UNIT // 2
 FLOPS = 3 * 2 * 512 * 512 * 512
 CHUNKS = ((0, 256), (256, 384), (384, 512))
 SUM_BANKS = (6, 7, 0, 1)
-OUT_BANKS = (2, 3, 4)
+GATE_BANKS = (6, 7, 0, 3)
+OUT_BANKS = (2, 1, 4)
 RAW_AT, W1Q_AT, W2Q_AT, Z_AT, RING_AT = 0, 4096, 6144, 9216, 13312
 
 
@@ -170,7 +171,7 @@ def tile_picked_glutap_none_po_kernel(
             nc.scalar.activation(dst[:], sum_bank[u][:], SIGMOID)
 
         def gate_back(u):
-            gate[u] = bank(SUM_BANKS[u], [P, PACK, UNIT])
+            gate[u] = bank(GATE_BANKS[u], [P, PACK, UNIT])
             for t in range(PACK):
                 nc.tensor.transpose(gate[u][:, t, :], gate_turned[u][:, t, :], ident[:])
 
@@ -350,11 +351,11 @@ def tile_picked_glutap_none_po_kernel(
             quantise_z(u)
         gather_e_apart(1)
         squash(3, turns.tile([P, PACK, P], F32, name="gate_turned3", offset=Z_AT - 8 * UNIT, align_bytes=64))
-        for u in (0, 1):
-            last_layer(u)
-        gate_back(3)
-        warm_up(1, 7)
+        last_layer(0)
         empty_bank(0)
+        gate_back(3)
+        last_layer(1)
+        warm_up(1, OUT_BANKS[0])
         gated(1, 2)
         for t in range(PACK):
             gather_e(2, t)

from contextlib import ExitStack

import concourse.mybir as mybir
from concourse.masks import make_identity

F32 = mybir.dt.float32
BF16 = mybir.dt.bfloat16
I32 = mybir.dt.int32
U32 = mybir.dt.uint32
U16 = mybir.dt.uint16
U8 = mybir.dt.uint8
FP8X4 = mybir.dt.float8_e4m3fn_x4
ADD = mybir.AluOpType.add
MULT = mybir.AluOpType.mult
SIGMOID = mybir.ActivationFunctionType.Sigmoid
COPY = mybir.ActivationFunctionType.Copy

P = 128
PACK = 4
T, S, H = 2048, 512, 512
HALF = S // 2
UNIT = 128
PIECE = UNIT // 2
FLOPS = 3 * 2 * 512 * 512 * 512
CHUNKS = ((0, 256), (256, 384), (384, 512))
SUM_BANKS = (6, 7, 0, 1)
GATE_BANKS = (6, 7, 0, 3)
OUT_BANKS = (2, 1, 4)
RAW_AT, W1Q_AT, W2Q_AT, Z_AT, RING_AT = 0, 4096, 6144, 9216, 13312


def tile_picked_glutap_none_po_kernel(
    tc, x_words, x_scales, w1_words, w1_scales, w2, w3_words, w3_scales, offs, tap, out_0, out_1, out_2
):
    nc = tc.nc
    with ExitStack() as ctx:
        keep = ctx.enter_context(tc.tile_pool(name="keep", bufs=1))
        turns = ctx.enter_context(tc.tile_pool(name="turns", bufs=1))
        late = ctx.enter_context(tc.tile_pool(name="late", bufs=1))
        psum = ctx.enter_context(tc.psum_pool(name="psum", bufs=1))

        def sb(name, shape, dtype):
            return keep.tile(shape, dtype, name=name, align_bytes=64)

        def bank(k, shape):
            return psum.tile(shape, F32, name=f"bank{k}")

        def words_view(dram):
            return dram[0].rearrange("p n t -> p (n t)").bitcast(I32)

        def load_scale_rows(queue, plane, dram):
            for r in range(4):
                queue.dma_start(plane[r:P:32, :].bitcast(I32), dram[0, r:16:4, :].bitcast(I32))

        def entries(lists, a, b):
            return lists[:, a // 16 : b // 16]

        offs_sb = keep.tile([P, S // 16], U16, name="offs_sb")
        tap_sb = keep.tile([P, S // 16], U16, name="tap_sb")
        x_tab = sb("x_tab", [P, T], U32)
        xs_tab = sb("xs_tab", [P, T], U8)
        w1s = sb("w1s", [P, PACK, P], U8)
        xs = sb("xs", [P, S], U8)
        w1_raw = sb("w1_raw", [P, H], U32)
        w3_raw = sb("w3_raw", [P, H], U32)
        w1s_raw = sb("w1s_raw", [P, H], U8)
        w3s_raw = sb("w3s_raw", [P, H], U8)
        w2_raw = [
            sb("w2_raw0", [P, PACK, H // 2], F32),
            turns.tile([P, PACK, H // 2], F32, name="w2_raw1", offset=RAW_AT, align_bytes=64),
        ]
        warm_out = sb("warm_out", [P, 16], F32)
        ident = sb("ident", [P, P], F32)

        nc.vector.memset(xs_tab[:].bitcast(I32), 0)
        nc.gpsimd.memset(w1s_raw[:].bitcast(I32), 0)
        nc.gpsimd.memset(w3s_raw[:].bitcast(I32), 0)
        make_identity(nc, ident[:])

        w2_rows = w2.rearrange("(p j) c -> p j c", j=PACK)
        nc.sync.dma_start(w1_raw[:].bitcast(I32), words_view(w1_words))
        nc.sync.dma_start(offs_sb[:], offs)
        for r in range(4):
            queue = nc.sync if r < 2 else nc.scalar
            queue.dma_start(xs_tab[r:P:32, :].bitcast(I32), x_scales[0, r:16:4, :].bitcast(I32))
        nc.sync.dma_start(x_tab[:].bitcast(I32), words_view(x_words))
        nc.scalar.activation(warm_out[:], ident[:, 0:16], SIGMOID)

        w1q = turns.tile([P, PACK, P], U32, name="w1q", offset=W1Q_AT, align_bytes=64)
        nc.vector.tensor_copy(w1q[:].rearrange("p t m -> p m t"), w1_raw[:].rearrange("p (m t) -> p m t", t=PACK))
        nc.vector.tensor_copy(xs[:], xs_tab[:].indirect(offs_sb[:]))
        load_scale_rows(nc.sync, w1s_raw, w1_scales)
        w1s_slices = w1s_raw[:].rearrange("p (m t) -> p t m", t=PACK)
        for t0, t1 in ((0, 1), (1, PACK)):
            nc.gpsimd.tensor_copy(w1s[:, t0:t1, :], w1s_slices[:, t0:t1, :])
        nc.sync.dma_start(w2_raw[0][:], w2_rows[:, :, 0 : H // 2])
        nc.sync.dma_start(tap_sb[:], tap)
        nc.sync.dma_start(w2_raw[1][:], w2_rows[:, :, H // 2 : H])
        nc.sync.dma_start(w3_raw[:].bitcast(I32), words_view(w3_words))
        load_scale_rows(nc.sync, w3s_raw, w3_scales)

        xq = sb("xq", [P, S], U32)
        for a, b in CHUNKS:
            nc.vector.tensor_copy(xq[:, a:b], x_tab[:].indirect(entries(offs_sb, a, b)))

        def project(wq, ws, t, a, b, k):
            acc = bank(k, [P, S])
            nc.tensor.matmul_mx(
                acc[:, 0 : b - a],
                lhsT=wq[:, t, :].bitcast(FP8X4),
                lhsT_scale=ws[:, t, :],
                rhs=xq[:, a:b].bitcast(FP8X4),
                rhs_scale=xs[:, a:b],
                start=True,
                stop=True,
            )
            return acc

        w2_bf = late.tile([P, PACK, P, PACK], BF16, name="w2_bf", offset=0, align_bytes=64)

        def w2_views(h):
            m0 = h * P // 2
            return (
                w2_bf[:, :, m0 : m0 + P // 2, :].rearrange("p t m j -> p m t j"),
                w2_raw[h][:].rearrange("p j (m t) -> p m t j", t=PACK),
            )

        y_win = [sb(f"y_win{t}", [P, S], F32) for t in range(PACK)]
        for k, (a, b) in enumerate(CHUNKS):
            acc = project(w1q, w1s, 0, a, b, k)
            nc.scalar.copy(y_win[0][:, a:b], acc[:, 0 : b - a])
        for t in range(1, PACK):
            acc = project(w1q, w1s, t, 0, S, 2 + t)
            nc.scalar.copy(y_win[t][:], acc[:])
        nc.vector.tensor_copy(*w2_views(0))
        nc.gpsimd.tensor_scalar(*w2_views(1), 1.0, 0.0, MULT, ADD)

        y_tap = {}
        sum_bank = {}
        gate_turned = {}
        gate = {}

        def cols(u):
            return slice(u * UNIT, (u + 1) * UNIT)

        turned = {u: 0 for u in range(PACK)}

        def add_turned(u, t, src):
            if turned[u] == 0:
                sum_bank[u] = bank(SUM_BANKS[u], [P, PACK, P])
            nc.tensor.matmul(
                sum_bank[u][:, t, :],
                src,
                ident[:],
                start=(turned[u] == 0),
                stop=(turned[u] == 2 * PACK - 1),
                is_transpose=True,
            )
            turned[u] = turned[u] + 1

        def turn_plain(t):
            for u in range(PACK):
                add_turned(u, t, y_win[t][:, cols(u)])

        def turn_taps(t, *some_units):
            for u in some_units:
                add_turned(u, t, y_tap[t, u])

        def squash(u, dst):
            gate_turned[u] = dst
            nc.scalar.activation(dst[:], sum_bank[u][:], SIGMOID)

        def gate_back(u):
            gate[u] = bank(GATE_BANKS[u], [P, PACK, UNIT])
            for t in range(PACK):
                nc.tensor.transpose(gate[u][:, t, :], gate_turned[u][:, t, :], ident[:])

        def gather_low(t, low):
            nc.vector.tensor_copy(low[:], y_win[t][:].indirect(entries(tap_sb, 0, HALF)))
            y_tap[t, 0], y_tap[t, 1] = low[:, cols(0)], low[:, cols(1)]

        def gather_third(t, third):
            u = 2 if t < 3 else 3
            nc.vector.tensor_copy(third[:], y_win[t][:].indirect(entries(tap_sb, u * UNIT, (u + 1) * UNIT)))
            y_tap[t, u] = third[:]

        gather_low(0, sb("y_low0", [P, HALF], F32))
        gather_third(0, sb("y_third0", [P, UNIT], F32))
        gather_low(1, sb("y_low1", [P, HALF], F32))
        for t in range(PACK):
            last = turns.tile([P, UNIT], F32, name=f"y_last{t}", offset=W1Q_AT + 4 * UNIT * t, align_bytes=64)
            u = 3 if t < 3 else 2
            nc.scalar.activation(last[:], y_win[t][:].indirect(entries(tap_sb, u * UNIT, (u + 1) * UNIT)), COPY)
            y_tap[t, u] = last[:]
        turn_plain(0)
        turn_taps(0, 0, 1, 2)
        turn_plain(1)
        turn_taps(1, 0, 1)
        turn_plain(2)

        w2q = turns.tile([P, PACK, P], U32, name="w2q", offset=W2Q_AT, align_bytes=64)
        w2s = sb("w2s", [P, PACK, P], U8)
        nc.vector.quantize_mx(
            out=w2q[:].rearrange("p t m -> p (t m)").bitcast(FP8X4),
            scales=w2s[:].rearrange("p t m -> p (t m)"),
            in_=w2_bf[:].rearrange("p t m j -> p (t m j)"),
        )
        e_acc = [project(w2q, w2s, t, 0, S, 2 + t) for t in range(PACK)]
        for t in (2, 3):
            gather_low(t, turns.tile([P, HALF], F32, name=f"y_low{t}", offset=RAW_AT + 4 * HALF * t, align_bytes=64))
        for t in range(1, PACK):
            gather_third(t, turns.tile([P, UNIT], F32, name=f"y_third{t}", offset=RAW_AT + 4 * UNIT * t, align_bytes=64))
        w3q = late.tile([P, PACK, P], U32, name="w3q", offset=0, align_bytes=64)
        w3s = late.tile([P, PACK, P], U8, name="w3s", offset=4 * H, align_bytes=64)
        for dealt, raw in ((w3s, w3s_raw), (w3q, w3_raw)):
            nc.gpsimd.tensor_copy(dealt[:], raw[:].rearrange("p (m t) -> p t m", t=PACK))

        e_win = [sb(f"e_win{t}", [P, S], F32) for t in range(PACK)]
        e_rows = turns.tile([P, 29, UNIT], F32, name="e_rows", offset=RING_AT, align_bytes=64)
        e_low = [sb(f"e_low{t}", [P, HALF], F32)[:] for t in range(PACK)]
        e_high_all = sb("e_high", [P, PACK, HALF], F32)
        e_high = [e_high_all[:, t, :] for t in range(PACK)]

        def window_e(t, copy):
            copy(e_win[t][:], e_acc[t][:])
            nc.sync.dma_start(e_high[t], e_win[t][:, HALF:S])

        def twin_e(t):
            nc.scalar.copy(e_low[t], e_acc[t][:, 0:HALF])

        for u, order in enumerate(((2, 3), (2, 3), (1, 2, 3), (3, 0, 1, 2))):
            turn_taps(order[0], u)
            add_turned(u, 3, y_win[3][:, cols(u)])
            for t in order[1:]:
                turn_taps(t, u)
        window_e(0, nc.scalar.copy)
        twin_e(1)
        twin_e(0)
        window_e(1, nc.vector.tensor_copy)
        window_e(2, nc.scalar.copy)
        twin_e(2)
        squash(0, sb("gate_turned0", [P, PACK, P], F32))
        window_e(3, nc.scalar.copy)
        twin_e(3)
        gate_back(0)
        squash(1, turns.tile([P, PACK, P], F32, name="gate_turned1", offset=W2Q_AT, align_bytes=64))
        squash(2, sb("gate_turned2", [P, PACK, P], F32))
        gate_back(1)
        gate_back(2)

        e_sum = [e_rows[:, 1:9, :].rearrange("p (t h) n -> p t (h n)", h=2), e_rows[:, 25:29, :], e_rows[:, 0:25:8, :]]

        oq = sb("oq", [P, S], U32)
        osc = sb("osc", [P, S], U8)
        out_rows = out_0.rearrange("(p t) n -> p t n", t=PACK)
        out_words = words_view(out_1)
        units = range(S // UNIT)
        z_bf = [turns.tile([P, UNIT, PACK], BF16, name=f"z_bf{u}", offset=Z_AT + 8 * UNIT * u, align_bytes=64) for u in units]
        zq = [sb(f"zq{u}", [P, UNIT], U32) for u in units]
        zs = [sb(f"zs{u}", [P, UNIT], U8) for u in units]
        o_bf = {u: sb(f"o_bf{u}", [P, UNIT, PACK], BF16) for u in (0, 2)}
        o_f32 = [sb(f"o_f32{u}", [P, PACK, UNIT], F32) for u in units]
        o_bank = {}

        def gather_e(c, t):
            a, b = CHUNKS[c]
            plain = e_low[t] if c == 0 else e_high[t][:, a - HALF : b - HALF]
            nc.vector.tensor_tensor(e_sum[c][:, t, :], e_win[t][:].indirect(entries(tap_sb, a, b)), plain, ADD)

        def gather_e_apart(c):
            a, b = CHUNKS[c]
            e_tap = e_rows[:, 12:25:4, :]
            for t in range(PACK):
                nc.scalar.activation(e_tap[:, t, :], e_win[t][:].indirect(entries(tap_sb, a, b)), COPY)
            nc.vector.tensor_tensor(e_sum[c], e_tap, e_high_all[:, :, a - HALF : b - HALF], ADD)

        def gated(c, u, a=0, b=UNIT):
            off = u * UNIT - CHUNKS[c][0]
            nc.vector.tensor_tensor(
                z_bf[u][:, a:b, :].rearrange("p (c i) t -> p c t i", i=4),
                e_sum[c][:, :, off + a : off + b].rearrange("p t (c i) -> p c t i", i=4),
                gate[u][:, :, a:b].rearrange("p t (c i) -> p c t i", i=4),
                MULT,
            )

        def quantise_z(u, a=0, b=UNIT):
            nc.vector.quantize_mx(
                out=zq[u][:, a:b].bitcast(FP8X4),
                scales=zs[u][:, a:b],
                in_=z_bf[u][:, a:b, :].rearrange("p n t -> p (n t)"),
            )

        def product(dst, t, u, a=0, b=UNIT):
            nc.tensor.matmul_mx(
                dst,
                lhsT=w3q[:, t, :].bitcast(FP8X4),
                lhsT_scale=w3s[:, t, :],
                rhs=zq[u][:, a:b].bitcast(FP8X4),
                rhs_scale=zs[u][:, a:b],
                start=True,
                stop=True,
            )

        def store_f32(u):
            nc.sync.dma_start(out_rows[:, :, u * UNIT : (u + 1) * UNIT], o_f32[u][:])

        def last_layer(u):
            o_bank[u] = bank(OUT_BANKS[u], [P, PACK, UNIT])
            for t in range(PACK):
                product(o_bank[u][:, t, :], t, u)
            nc.scalar.copy(o_f32[u][:], o_bank[u][:])
            store_f32(u)

        def empty_bank(u):
            nc.scalar.copy(o_bf[u][:], o_bank[u][:].rearrange("p t n -> p n t"))

        def round_walk(dst, src):
            nc.vector.tensor_copy(
                dst.rearrange("p (c i) t -> p c t i", i=4), src.rearrange("p t (c i) -> p c t i", i=4)
            )

        def last_piece(u, a, b, k):
            acc = bank(k, [P, PACK, b - a])
            for t in range(PACK):
                product(acc[:, t, :], t, u, a, b)
            round_walk(o_bf[u][:, a:b, :], acc[:])
            nc.scalar.copy(o_f32[u][:, :, a:b], acc[:])

        def warm_up(u, k):
            spare = bank(k, [P, S])
            nc.tensor.matmul_mx(
                spare[:],
                lhsT=zq[u][:].bitcast(FP8X4),
                lhsT_scale=zs[u][:],
                rhs=w3q[:].rearrange("p t m -> p (t m)").bitcast(FP8X4),
                rhs_scale=w3s[:].rearrange("p t m -> p (t m)"),
                start=True,
                stop=True,
            )

        def hand_on(u, a=0, b=UNIT):
            to = slice(u * UNIT + a, u * UNIT + b)
            nc.vector.quantize_mx(
                out=oq[:, to].bitcast(FP8X4), scales=osc[:, to], in_=o_bf[u][:, a:b, :].rearrange("p n t -> p (n t)")
            )

        for t in range(PACK):
            gather_e(0, t)
        for u in (0, 1):
            gated(0, u)
            quantise_z(u)
        gather_e_apart(1)
        squash(3, turns.tile([P, PACK, P], F32, name="gate_turned3", offset=Z_AT - 8 * UNIT, align_bytes=64))
        last_layer(0)
        empty_bank(0)
        gate_back(3)
        last_layer(1)
        warm_up(1, OUT_BANKS[0])
        gated(1, 2)
        for t in range(PACK):
            gather_e(2, t)
        quantise_z(2)
        last_layer(2)
        empty_bank(2)
        for a in (0, PIECE):
            gated(2, 3, a, a + PIECE)
            quantise_z(3, a, a + PIECE)
        hand_on(0)
        o_bf[1] = turns.tile([P, UNIT, PACK], BF16, name="o_bf1", offset=RING_AT, align_bytes=64)
        round_walk(o_bf[1][:], o_f32[1][:])
        hand_on(1)
        o_bf[3] = sb("o_bf0", [P, UNIT, PACK], BF16)
        last_piece(3, 0, PIECE, 5)
        last_piece(3, PIECE, UNIT, 6)
        nc.scalar.dma_start(out_rows[:, :, 3 * UNIT : S], o_f32[3][:])
        hand_on(2)
        for a in (0, PIECE):
            hand_on(3, a, a + PIECE)
        for a, b in ((0, HALF), (HALF, S)):
            nc.sync.dma_start(out_words[:, a:b], oq[:, a:b].bitcast(I32))
        for q in range(4):
            queue = nc.scalar if q >= 2 else nc.sync
            queue.dma_start(out_2[0, q:16:4, :].bitcast(I32), osc[q:P:32, :].bitcast(I32))
